import numpy as np
import ml_dtypes


def mxq(x, axis, fmt="e4m3"):
    dtype, down = {"e4m3": (ml_dtypes.float8_e4m3fn, 7), "e5m2": (ml_dtypes.float8_e5m2, 14)}[fmt]
    v = np.moveaxis(np.asarray(x, np.float32).astype(ml_dtypes.bfloat16).astype(np.float64), axis, -1)
    blocks = v.reshape(v.shape[:-1] + (-1, 32))
    amax = np.abs(blocks).max(-1, keepdims=True)
    byte = np.maximum(np.where(amax > 0, np.frexp(amax)[1] - 1 + 127, 0) - down, 1)
    scale = np.exp2(byte - 127.0)
    codes = (blocks / scale).astype(np.float32).astype(dtype).astype(np.float64)
    return np.moveaxis((codes * scale).reshape(v.shape), -1, axis)


WIDE = False


def mx_kscale(k):
    if not WIDE:
        return np.ones(k)
    levels = np.array([10, -10, 5, -5, 0])
    if k % 512:
        return np.exp2(np.random.permutation(np.resize(levels, k // 32))).repeat(32)
    a = np.empty((k // 512, 16))
    for p in range(k // 512):
        a[p, :8] = np.random.permutation(np.resize(levels, 8))
        for g in range(8):
            far = levels[np.abs(levels - a[p, g]) >= 10]
            a[p, g + 8] = far[np.random.randint(len(far))]
    return np.exp2(a.ravel()).repeat(32)


def f64(x):
    return np.asarray(x).astype(np.float64)


def striped(idx):
    return np.tile(idx.reshape(-1, 16).T, (8, 1)).astype(np.uint16)


def unstriped(offs):
    return offs[:16].T.reshape(-1).astype(np.int64)


E2M1 = np.array([0.0, 0.5, 1.0, 1.5, 2.0, 3.0, 4.0, 6.0, -0.0, -0.5, -1.0, -1.5, -2.0, -3.0, -4.0, -6.0])


def pack_weight(w, fmt):
    k, n = w.shape
    w = f64(np.asarray(w, np.float32).astype(ml_dtypes.bfloat16)).reshape(k // 32, 32, n)
    amax = np.abs(w).max(1)
    if fmt == "e4m3":
        byte = np.frexp(amax)[1] - 1 + 127 - 7
    else:
        mant, ex = np.frexp(amax / 6.0)
        byte = np.where(mant > 0.5, ex, ex - 1) + 127
    byte = np.clip(np.where(amax > 0, byte, 1), 1, 254)
    scaled = (w * np.exp2(127.0 - byte)[:, None, :]).reshape(k, n).astype(np.float32)
    by_word = np.ascontiguousarray(scaled.reshape(k // 512, 128, 4, n).transpose(0, 1, 3, 2))
    if fmt == "e4m3":
        words = by_word.astype(ml_dtypes.float8_e4m3fn).view(np.uint8)
    else:
        c = by_word.astype(ml_dtypes.float4_e2m1fn).view(np.uint8) & 0xF
        words = (c[..., 0::2] | (c[..., 1::2] << 4)).reshape(k // 512, 128, 2 * n)
    return np.ascontiguousarray(words), np.ascontiguousarray(byte.astype(np.uint8).reshape(k // 512, 16, n))


def unpack_weight(words, scales, fmt):
    g, _, n = scales.shape
    words = np.ascontiguousarray(words).reshape(g, 128, n, -1)
    if fmt == "e4m3":
        vals = words.view(ml_dtypes.float8_e4m3fn).astype(np.float64)
    else:
        nib = np.empty((g, 128, n, 4), np.uint8)
        nib[..., 0::2] = words & 0xF
        nib[..., 1::2] = words >> 4
        vals = E2M1[nib]
    vals = vals * np.repeat(np.exp2(scales.astype(np.float64) - 127.0), 8, axis=1)[..., None]
    return vals.transpose(0, 1, 3, 2).reshape(g * 512, n)


def gelu(v):
    return 0.5 * v * (1.0 + np.tanh(np.sqrt(2.0 / np.pi) * (v + 0.044715 * v**3)))


K, H, T, S, P = 512, 1024, 2048, 1024, 512

def setup_inputs():
    n = np.random.standard_normal
    s = mx_kscale(K)[:, None]
    u = mx_kscale(H)[:, None]
    tab_words, tab_scales = pack_weight(n((K, T)) * s, "e4m3")
    w2_words, w2_scales = pack_weight(n((K, H)) * 0.7 / np.sqrt(K) / s, "e4m3")
    w3_words, w3_scales = pack_weight(n((H, H)) * 0.8 / np.sqrt(H) / u, "e2m1")
    return {
        "tab_words": tab_words, "tab_scales": tab_scales,
        "offs": striped(np.random.permutation(T)[:S]),
        "pos1": striped(np.random.permutation(S)[:P]),
        "w1": (n((K, H)) * 1.6 / np.sqrt(K) / s).astype(np.float32),
        "w2_words": w2_words, "w2_scales": w2_scales,
        "gain": (np.exp(0.3 * n(H)) * u[:, 0]).astype(np.float32),
        "lap": (n((H, P)) * u).astype(np.float32),
        "w3_words": w3_words, "w3_scales": w3_scales,
        "w4": (n((H, H)) * 0.6 / np.sqrt(H) / u).astype(np.float32),
        "skip": (np.exp(0.3 * n(H)) / u[:, 0]).astype(np.float32),
        "wgo": np.exp(0.3 * n((128, P))).astype(np.float32),
    }

def reference(tab_words, tab_scales, offs, pos1, w1, w2_words, w2_scales, gain, lap, w3_words, w3_scales, w4, skip, wgo):
    v = unpack_weight(tab_words, tab_scales, "e4m3")[:, unstriped(offs)]
    w2 = unpack_weight(w2_words, w2_scales, "e4m3")
    w3 = unpack_weight(w3_words, w3_scales, "e2m1")
    bent = np.tanh(mxq(f64(w1), 0, "e4m3").T @ v)
    h = f64(gain)[:, None] * (bent + (w2.T @ v))
    hp = h[:, unstriped(pos1)]
    x1 = mxq(np.abs(hp), 0, "e4m3")
    x2 = mxq(hp + f64(lap), 0, "e4m3")
    both = w3.T @ x1 + mxq(f64(w4), 0, "e4m3").T @ x2
    out = f64(skip)[:, None] * h
    y = both * out[:, unstriped(pos1)]
    out[:, unstriped(pos1)] = np.tile(f64(wgo), (H // 128, 1)) * y
    return out

@@ -1,0 +1,256 @@
+from contextlib import ExitStack
+
+import concourse.mybir as mybir
+
+K, H, T, S, NP = 512, 1024, 2048, 1024, 512
+FLOPS = 2 * (2 * K * H * S + 2 * H * H * NP)
+
+F32 = mybir.dt.float32
+BF16 = mybir.dt.bfloat16
+I32 = mybir.dt.int32
+U32 = mybir.dt.uint32
+U16 = mybir.dt.uint16
+U8 = mybir.dt.uint8
+FP8X4 = mybir.dt.float8_e4m3fn_x4
+FP4X4 = mybir.dt.float4_e2m1fn_x4
+ACT = mybir.ActivationFunctionType
+MULT = mybir.AluOpType.mult
+ADD = mybir.AluOpType.add
+
+P = 128
+PACK = 4
+KP = P * PACK
+NB = H // KP
+BANK = 512
+HALF = NP // 2
+
+
+def tile_list_tricot_lapping_inspector_kernel(
+    tc, tab_words, tab_scales, offs, pos1, w1, w2_words, w2_scales, gain, lap, w3_words, w3_scales, w4, skip, wgo, out
+):
+    nc = tc.nc
+    with ExitStack() as ctx:
+        keep = ctx.enter_context(tc.tile_pool(name="keep", bufs=1))
+        raw = ctx.enter_context(tc.tile_pool(name="raw", bufs=4))
+        ring = ctx.enter_context(tc.tile_pool(name="ring", bufs=2))
+        ring3 = ctx.enter_context(tc.tile_pool(name="ring3", bufs=3))
+        ps1 = ctx.enter_context(tc.psum_pool(name="ps1", bufs=3))
+        ps2 = ctx.enter_context(tc.psum_pool(name="ps2", bufs=2))
+
+        def held(shape, dtype, name):
+            return keep.tile(shape, dtype, name=name, align_bytes=64)
+
+        idx = held([P, S // 16], U16, "idx")
+        pos = held([P, NP // 16], U16, "pos")
+        tabw = held([P, T], U32, "tabw")
+        tabs = held([P, T], U8, "tabs")
+        w2sc = held([P, H], U8, "w2sc")
+        w3sc = held([P, NB, H], U8, "w3sc")
+        w2w = [held([P, KP], U32, f"w2w{b}") for b in range(NB)]
+        w3w = [held([P, 2 * H], U8, f"w3w{a}") for a in range(NB)]
+        gain_c = held([P, NB, PACK], F32, "gain_c")
+        skip_c = held([P, NB, PACK], F32, "skip_c")
+        lap_t = [held([P, PACK, NP], F32, f"lap{b}") for b in range(NB)]
+        wgo_t = held([P, PACK, NP], F32, "wgo_t")
+
+        nc.gpsimd.memset(tabs[:].bitcast(I32), 0)
+        nc.gpsimd.memset(w2sc[:].bitcast(I32), 0)
+        nc.gpsimd.memset(w3sc[:].rearrange("p a c -> p (a c)").bitcast(I32), 0)
+
+        def load_scale_rows(eng, plane, rows, first):
+            for q in range(4):
+                eng.dma_start(
+                    plane[32 * q + first : 32 * q + first + 4, :].bitcast(I32),
+                    rows[4 * q : 4 * q + 4, :].bitcast(I32),
+                )
+
+        def load_weight(w, a, b):
+            piece = raw.tile([P, PACK, KP], F32, name="piece")
+            nc.sync.dma_start(
+                piece[:], w[a * KP : (a + 1) * KP, b * KP : (b + 1) * KP].rearrange("(p j) c -> p j c", j=PACK)
+            )
+            return piece
+
+        w2_all = w2_words[0].rearrange("p c i -> p (c i)")
+
+        nc.sync.dma_start(idx[:], offs)
+        nc.sync.dma_start(pos[:], pos1)
+        load_scale_rows(nc.sync, tabs, tab_scales[0], 0)
+        w1_raw = [load_weight(w1, 0, 0)]
+        nc.sync.dma_start(tabw[:].bitcast(I32), tab_words[0].rearrange("p c i -> p (c i)").bitcast(I32))
+        nc.sync.dma_start(w2w[0][:].bitcast(I32), w2_all[:, 0 : 4 * KP].bitcast(I32))
+        load_scale_rows(nc.sync, w2sc, w2_scales[0], 0)
+        nc.sync.dma_start(gain_c[:], gain.rearrange("(b p t) -> p b t", b=NB, t=PACK))
+        w1_raw.append(load_weight(w1, 0, 1))
+        nc.sync.dma_start(w2w[1][:].bitcast(I32), w2_all[:, 4 * KP : 8 * KP].bitcast(I32))
+        w4_raw = {(0, 0): load_weight(w4, 0, 0), (1, 0): load_weight(w4, 1, 0)}
+        for b in range(NB):
+            nc.sync.dma_start(lap_t[b][:], lap[b * KP : (b + 1) * KP, :].rearrange("(p t) m -> p t m", t=PACK))
+        nc.sync.dma_start(skip_c[:], skip.rearrange("(b p t) -> p b t", b=NB, t=PACK))
+        for q in range(4):
+            nc.sync.dma_start(
+                w3sc[32 * q : 32 * q + 4].bitcast(I32),
+                w3_scales[:, 4 * q : 4 * q + 4, :].rearrange("a q c -> q a c").bitcast(I32),
+            )
+        for a in range(NB):
+            nc.sync.dma_start(w3w[a][:].bitcast(I32), w3_words[a].bitcast(I32))
+        for q in range(4):
+            nc.sync.dma_start(wgo_t[32 * q : 32 * q + 32], wgo.rearrange("(p t) m -> p t m", t=PACK))
+        for a in range(NB):
+            w4_raw[(a, 1)] = load_weight(w4, a, 1)
+
+        vs = held([P, S], U8, "vs")
+        nc.vector.tensor_copy(vs[:], tabs[:].indirect(idx[:]))
+
+        def deal(eng, dst, src):
+            eng(
+                dst.rearrange("p (b t m) -> p b m t", t=PACK, m=P),
+                src.rearrange("p (b m t) -> p b m t", t=PACK, m=P),
+            )
+
+        def round_weight(piece, share=0):
+            staged = ring.tile([P, PACK * KP], BF16, name="staged", align_bytes=64)
+            dst = staged[:].rearrange("p (t m j) -> p m j t", t=PACK, j=PACK)
+            src = piece[:].rearrange("p j (m t) -> p m j t", t=PACK)
+            nc.scalar.copy(dst[:, share:], src[:, share:])
+            if share:
+                nc.vector.tensor_copy(dst[:, :share], src[:, :share])
+            return staged
+
+        def quantise(staged, width, name):
+            codes = held([P, width], U32, name + "c")
+            scales = held([P, width], U8, name + "s")
+            nc.vector.quantize_mx(out=codes[:].bitcast(FP8X4), scales=scales[:], in_=staged[:])
+            return codes, scales
+
+        w2scd = held([P, H], U8, "w2scd")
+        w3scd = held([P, NB * H], U8, "w3scd")
+        w2d = [held([P, KP], U32, f"w2d{b}") for b in range(NB)]
+        w3d = [held([P, 2 * H], U8, f"w3d{a}") for a in range(NB)]
+
+        h = {}
+        hp = [held([P, PACK, NP], F32, f"hp{b}") for b in range(NB)]
+        w1q, w4q, x1q, x2q = {}, {}, {}, {}
+
+        def first_stage(b, t):
+            h[(b, t)] = held([P, S], F32, f"h{b}{t}")
+            cols = slice(t * P, (t + 1) * P)
+            g = gain_c[:, b, t : t + 1]
+            for jh in range(2):
+                js = slice(jh * BANK, (jh + 1) * BANK)
+                pa = ps1.tile([P, BANK], F32, name="pa")
+                pb = ps1.tile([P, BANK], F32, name="pb")
+                nc.tensor.matmul_mx(
+                    out=pa[:], lhsT=w1q[b][0][:, cols].bitcast(FP8X4), lhsT_scale=w1q[b][1][:, cols],
+                    rhs=vw[jh][:].bitcast(FP8X4), rhs_scale=vs[:, js], start=True, stop=True,
+                )
+                nc.tensor.matmul_mx(
+                    out=pb[:], lhsT=w2d[b][:, cols].bitcast(FP8X4),
+                    lhsT_scale=w2scd[:, b * KP + t * P : b * KP + (t + 1) * P],
+                    rhs=vw[jh][:].bitcast(FP8X4), rhs_scale=vs[:, js], start=True, stop=True,
+                )
+                bent = ring3.tile([P, BANK], F32, name="bent")
+                nc.scalar.activation(bent[:], pa[:], ACT.Tanh)
+                gbent = ring3.tile([P, BANK], F32, name="gbent")
+                nc.scalar.activation(gbent[:], bent[:], ACT.Copy, scale=g)
+                nc.vector.scalar_tensor_tensor(h[(b, t)][:, js], pb[:], g, gbent[:], MULT, ADD)
+
+        def pick(b, t):
+            nc.vector.tensor_copy(hp[b][:, t, :], h[(b, t)][:].indirect(pos[:]))
+
+        def second_operands(hf, b):
+            walk_out = "p (c i t) -> p c t i"
+            walk_in = "p t (c i) -> p c t i"
+            picked = hp[b][:, :, hf * HALF : (hf + 1) * HALF].rearrange(walk_in, i=4)
+            s1 = ring.tile([P, PACK * HALF], BF16, name="s1", align_bytes=64)
+            nc.scalar.activation(s1[:].rearrange(walk_out, i=4, t=PACK), picked, ACT.Abs)
+            s2 = ring.tile([P, PACK * HALF], BF16, name="s2", align_bytes=64)
+            nc.vector.tensor_tensor(
+                s2[:].rearrange(walk_out, i=4, t=PACK), picked,
+                lap_t[b][:, :, hf * HALF : (hf + 1) * HALF].rearrange(walk_in, i=4), ADD,
+            )
+            x2q[(hf, b)] = quantise(s2, HALF, f"x2{hf}{b}")
+            x1q[(hf, b)] = quantise(s1, HALF, f"x1{hf}{b}")
+
+        res = {}
+
+        def scale_all(b, t):
+            res[(b, t)] = held([P, S], F32, f"res{b}{t}")
+            nc.scalar.activation(res[(b, t)][:], h[(b, t)][:], ACT.Copy, scale=skip_c[:, b, t : t + 1])
+
+        def second_stage(hf, b, t):
+            both = ps2.tile([P, HALF], F32, name="both")
+            c0 = b * KP + t * P
+            for a in range(NB):
+                nc.tensor.matmul_mx(
+                    out=both[:], lhsT=w4q[(a, b)][0][:, t * P : (t + 1) * P].bitcast(FP8X4),
+                    lhsT_scale=w4q[(a, b)][1][:, t * P : (t + 1) * P],
+                    rhs=x2q[(hf, a)][0][:].bitcast(FP8X4), rhs_scale=x2q[(hf, a)][1][:],
+                    start=(a == 0), stop=False,
+                )
+                nc.tensor.matmul_mx(
+                    out=both[:], lhsT=w3d[a][:, 2 * c0 : 2 * (c0 + P)].bitcast(FP4X4),
+                    lhsT_scale=w3scd[:, a * H + c0 : a * H + c0 + P],
+                    rhs=x1q[(hf, a)][0][:].bitcast(FP8X4), rhs_scale=x1q[(hf, a)][1][:],
+                    start=False, stop=(a == NB - 1),
+                )
+            y = ring3.tile([P, HALF], F32, name="y")
+            nc.vector.scalar_tensor_tensor(y[:], both[:], skip_c[:, b, t : t + 1], hp[b][:, t, hf * HALF : (hf + 1) * HALF], MULT, MULT)
+            return y
+
+        def put(hf, b, t, y):
+            nc.vector.tensor_tensor(
+                res[(b, t)][:].indirect(pos[:, hf * 16 : (hf + 1) * 16]), y[:],
+                wgo_t[:, t, hf * HALF : (hf + 1) * HALF], MULT,
+            )
+
+        tiles = [(b, t) for b in range(NB) for t in range(PACK)]
+        w1q[0] = quantise(round_weight(w1_raw[0], 64), KP, "w1q0")
+        vw = []
+        for jh in range(2):
+            words = held([P, BANK], U32, f"vw{jh}")
+            nc.vector.tensor_copy(words[:], tabw[:].indirect(idx[:, jh * 32 : (jh + 1) * 32]))
+            vw.append(words)
+            if jh == 0:
+                deal(nc.vector.tensor_copy, w2scd[:], w2sc[:])
+                deal(nc.vector.tensor_copy, w2d[0][:].bitcast(I32), w2w[0][:].bitcast(I32))
+        for i, (b, t) in enumerate(tiles):
+            first_stage(b, t)
+            if i > 0:
+                pick(*tiles[i - 1])
+            if i == 1:
+                w1q[1] = quantise(round_weight(w1_raw[1]), KP, "w1q1")
+                deal(nc.vector.tensor_copy, w2d[1][:].bitcast(I32), w2w[1][:].bitcast(I32))
+            if i == 4:
+                w4q[(0, 0)] = quantise(round_weight(w4_raw[(0, 0)]), KP, "w4q00")
+            if i == 5:
+                second_operands(0, 0)
+            if i == 6:
+                w4q[(1, 0)] = quantise(round_weight(w4_raw[(1, 0)]), KP, "w4q10")
+        pick(*tiles[-1])
+        second_operands(0, 1)
+        deal(nc.vector.tensor_copy, w3scd[:], w3sc[:].rearrange("p a c -> p (a c)"))
+        for a in range(NB):
+            deal(nc.scalar.copy, w3d[a][:].bitcast(U16), w3w[a][:].bitcast(U16))
+
+        out_rows = out.rearrange("(b p t) j -> b t p j", b=NB, t=PACK)
+        steps = [(hf, b, t) for hf in range(2) for (b, t) in tiles]
+        ys = {}
+        for n, (hf, b, t) in enumerate(steps):
+            if hf == 0:
+                scale_all(b, t)
+            ys[n] = second_stage(hf, b, t)
+            if n == 0:
+                second_operands(1, 0)
+            if n == 1:
+                w4q[(0, 1)] = quantise(round_weight(w4_raw[(0, 1)]), KP, "w4q01")
+            if n == 2:
+                w4q[(1, 1)] = quantise(round_weight(w4_raw[(1, 1)]), KP, "w4q11")
+            if n == 4:
+                second_operands(1, 1)
+            if n > 0:
+                put(*steps[n - 1], ys[n - 1])
+                if steps[n - 1][0] == 1:
+                    nc.sync.dma_start(out_rows[steps[n - 1][1], steps[n - 1][2]], res[steps[n - 1][1:]][:])
+        put(*steps[-1], ys[len(steps) - 1])
+        nc.sync.dma_start(out_rows[steps[-1][1], steps[-1][2]], res[steps[-1][1:]][:])

@@ -23,6 +23,11 @@ KP = P * PACK
 NB = H // KP
 BANK = 512
 HALF = NP // 2
+PAIR = 2 * P
+UWIN = False
+X2G = ()
+W3W = "S"
+W3S = "V"
 
 
 def tile_list_tricot_lapping_inspector_kernel(
@@ -31,11 +36,12 @@ def tile_list_tricot_lapping_inspector_kernel(
     nc = tc.nc
     with ExitStack() as ctx:
         keep = ctx.enter_context(tc.tile_pool(name="keep", bufs=1))
-        raw = ctx.enter_context(tc.tile_pool(name="raw", bufs=4))
+        raw = ctx.enter_context(tc.tile_pool(name="raw", bufs=3))
         ring = ctx.enter_context(tc.tile_pool(name="ring", bufs=2))
         ring3 = ctx.enter_context(tc.tile_pool(name="ring3", bufs=3))
         ps1 = ctx.enter_context(tc.psum_pool(name="ps1", bufs=3))
         ps2 = ctx.enter_context(tc.psum_pool(name="ps2", bufs=2))
+        movers = {"S": nc.scalar.copy, "V": nc.vector.tensor_copy, "G": nc.gpsimd.tensor_copy}
 
         def held(shape, dtype, name):
             return keep.tile(shape, dtype, name=name, align_bytes=64)
@@ -47,9 +53,9 @@ def tile_list_tricot_lapping_inspector_kernel(
         w2sc = held([P, H], U8, "w2sc")
         w3sc = held([P, NB, H], U8, "w3sc")
         w2w = [held([P, KP], U32, f"w2w{b}") for b in range(NB)]
-        w3w = [held([P, 2 * H], U8, f"w3w{a}") for a in range(NB)]
-        gain_c = held([P, NB, PACK], F32, "gain_c")
-        skip_c = held([P, NB, PACK], F32, "skip_c")
+        w3w = held([P, NB, 2 * H], U8, "w3w")
+        gain_c = held([P, NB * PACK], F32, "gain_c")
+        skip_c = held([P, NB * PACK], F32, "skip_c")
         lap_t = [held([P, PACK, NP], F32, f"lap{b}") for b in range(NB)]
         wgo_t = held([P, PACK, NP], F32, "wgo_t")
 
@@ -57,12 +63,9 @@ def tile_list_tricot_lapping_inspector_kernel(
         nc.gpsimd.memset(w2sc[:].bitcast(I32), 0)
         nc.gpsimd.memset(w3sc[:].rearrange("p a c -> p (a c)").bitcast(I32), 0)
 
-        def load_scale_rows(eng, plane, rows, first):
-            for q in range(4):
-                eng.dma_start(
-                    plane[32 * q + first : 32 * q + first + 4, :].bitcast(I32),
-                    rows[4 * q : 4 * q + 4, :].bitcast(I32),
-                )
+        def load_scale_rows(plane, rows, quads):
+            for q in quads:
+                nc.sync.dma_start(plane[32 * q : 32 * q + 4, :].bitcast(I32), rows[4 * q : 4 * q + 4, :].bitcast(I32))
 
         def load_weight(w, a, b):
             piece = raw.tile([P, PACK, KP], F32, name="piece")
@@ -71,51 +74,44 @@ def tile_list_tricot_lapping_inspector_kernel(
             )
             return piece
 
+        def load_rows(cols, vec):
+            nc.sync.dma_start(
+                cols[:].rearrange("p (b t) -> p b t", b=NB), vec.rearrange("(b p t) -> p b t", b=NB, t=PACK)
+            )
+
         w2_all = w2_words[0].rearrange("p c i -> p (c i)")
 
         nc.sync.dma_start(idx[:], offs)
         nc.sync.dma_start(pos[:], pos1)
-        load_scale_rows(nc.sync, tabs, tab_scales[0], 0)
-        w1_raw = [load_weight(w1, 0, 0)]
+        load_scale_rows(tabs, tab_scales[0], range(4))
         nc.sync.dma_start(tabw[:].bitcast(I32), tab_words[0].rearrange("p c i -> p (c i)").bitcast(I32))
+        load_scale_rows(w2sc, w2_scales[0], range(1))
+        w1_raw = [load_weight(w1, 0, 0)]
         nc.sync.dma_start(w2w[0][:].bitcast(I32), w2_all[:, 0 : 4 * KP].bitcast(I32))
-        load_scale_rows(nc.sync, w2sc, w2_scales[0], 0)
-        nc.sync.dma_start(gain_c[:], gain.rearrange("(b p t) -> p b t", b=NB, t=PACK))
-        w1_raw.append(load_weight(w1, 0, 1))
-        nc.sync.dma_start(w2w[1][:].bitcast(I32), w2_all[:, 4 * KP : 8 * KP].bitcast(I32))
-        w4_raw = {(0, 0): load_weight(w4, 0, 0), (1, 0): load_weight(w4, 1, 0)}
-        for b in range(NB):
-            nc.sync.dma_start(lap_t[b][:], lap[b * KP : (b + 1) * KP, :].rearrange("(p t) m -> p t m", t=PACK))
-        nc.sync.dma_start(skip_c[:], skip.rearrange("(b p t) -> p b t", b=NB, t=PACK))
+        load_scale_rows(w2sc, w2_scales[0], range(1, 4))
+        load_rows(gain_c, gain)
         for q in range(4):
-            nc.sync.dma_start(
+            (nc.gpsimd if q > 1 else nc.sync).dma_start(
                 w3sc[32 * q : 32 * q + 4].bitcast(I32),
                 w3_scales[:, 4 * q : 4 * q + 4, :].rearrange("a q c -> q a c").bitcast(I32),
             )
-        for a in range(NB):
-            nc.sync.dma_start(w3w[a][:].bitcast(I32), w3_words[a].bitcast(I32))
+        w1_raw.append(load_weight(w1, 0, 1))
         for q in range(4):
             nc.sync.dma_start(wgo_t[32 * q : 32 * q + 32], wgo.rearrange("(p t) m -> p t m", t=PACK))
+        nc.sync.dma_start(w2w[1][:].bitcast(I32), w2_all[:, 4 * KP : 8 * KP].bitcast(I32))
+        load_rows(skip_c, skip)
+        nc.sync.dma_start(lap_t[0][:], lap[0:KP, :].rearrange("(p t) m -> p t m", t=PACK))
+        w4_raw = {(a, 0): load_weight(w4, a, 0) for a in range(NB)}
+        nc.sync.dma_start(w3w[:].bitcast(I32), w3_words.rearrange("a p c -> p a c").bitcast(I32))
+        nc.sync.dma_start(lap_t[1][:], lap[KP : 2 * KP, :].rearrange("(p t) m -> p t m", t=PACK))
         for a in range(NB):
             w4_raw[(a, 1)] = load_weight(w4, a, 1)
 
         vs = held([P, S], U8, "vs")
         nc.vector.tensor_copy(vs[:], tabs[:].indirect(idx[:]))
 
-        def deal(eng, dst, src):
-            eng(
-                dst.rearrange("p (b t m) -> p b m t", t=PACK, m=P),
-                src.rearrange("p (b m t) -> p b m t", t=PACK, m=P),
-            )
-
-        def round_weight(piece, share=0):
-            staged = ring.tile([P, PACK * KP], BF16, name="staged", align_bytes=64)
-            dst = staged[:].rearrange("p (t m j) -> p m j t", t=PACK, j=PACK)
-            src = piece[:].rearrange("p j (m t) -> p m j t", t=PACK)
-            nc.scalar.copy(dst[:, share:], src[:, share:])
-            if share:
-                nc.vector.tensor_copy(dst[:, :share], src[:, :share])
-            return staged
+        def deal(move, dst, src):
+            move(dst.rearrange("p a (t m) -> p a m t", t=PACK), src.rearrange("p a (m t) -> p a m t", t=PACK))
 
         def quantise(staged, width, name):
             codes = held([P, width], U32, name + "c")
@@ -123,49 +119,90 @@ def tile_list_tricot_lapping_inspector_kernel(
             nc.vector.quantize_mx(out=codes[:].bitcast(FP8X4), scales=scales[:], in_=staged[:])
             return codes, scales
 
-        w2scd = held([P, H], U8, "w2scd")
-        w3scd = held([P, NB * H], U8, "w3scd")
-        w2d = [held([P, KP], U32, f"w2d{b}") for b in range(NB)]
-        w3d = [held([P, 2 * H], U8, f"w3d{a}") for a in range(NB)]
+        def weight_pair(move, piece, tp, name):
+            staged = ring.tile([P, PACK * PAIR], BF16, name="staged", align_bytes=64, bufs=3)
+            move(
+                staged[:].rearrange("p (t m j) -> p m j t", t=2, j=PACK),
+                piece[:].rearrange("p j (m t) -> p m j t", t=PACK)[:, :, :, 2 * tp : 2 * tp + 2],
+            )
+            return quantise(staged, PAIR, name)
+
+        w2scd = [held([P, 1, KP], U8, f"w2scd{b}") for b in range(NB)]
+        w2d = [held([P, 1, KP], U32, f"w2d{b}") for b in range(NB)]
+        w3scd = [held([P, NB, KP], U8, f"w3scd{b}") for b in range(NB)]
+        w3d = [held([P, NB, 2 * KP], U8, f"w3d{b}") for b in range(NB)]
+
+        def deal_w2(b, move):
+            deal(nc.vector.tensor_copy, w2scd[b][:], w2sc[:, b * KP : (b + 1) * KP].rearrange("p (a c) -> p a c", a=1))
+            deal(move, w2d[b][:], w2w[b][:].rearrange("p (a c) -> p a c", a=1))
+
+        def deal_w3s(b):
+            deal(movers[W3S], w3scd[b][:], w3sc[:, :, b * KP : (b + 1) * KP])
+
+        def deal_w3(b):
+            deal(movers[W3W], w3d[b][:].bitcast(U16), w3w[:, :, 2 * b * KP : 2 * (b + 1) * KP].bitcast(U16))
 
         h = {}
-        hp = [held([P, PACK, NP], F32, f"hp{b}") for b in range(NB)]
+        hp = held([P, NB * PACK, NP], F32, "hp")
+        hw = {}
         w1q, w4q, x1q, x2q = {}, {}, {}, {}
+        both_c = skip_c
+        if UWIN:
+            both_c = held([P, NB * PACK], F32, "both_c")
+            nc.vector.tensor_tensor(both_c[:], gain_c[:], skip_c[:], MULT)
 
-        def first_stage(b, t):
+        def col(cols, b, t):
+            return cols[:, b * PACK + t : b * PACK + t + 1]
+
+        def pick(i):
+            b, t = tiles[i]
+            nc.vector.tensor_copy(hp[:, i, :], h[(b, t)][:].indirect(pos[:]))
+            hw[(b, t)] = held([P, NP], F32, f"hw{b}{t}")
+            nc.gpsimd.tensor_tensor(hw[(b, t)][:], hp[:, i, :], wgo_t[:, t, :], MULT)
+
+        def first_stage(i):
+            b, t = tiles[i]
             h[(b, t)] = held([P, S], F32, f"h{b}{t}")
-            cols = slice(t * P, (t + 1) * P)
-            g = gain_c[:, b, t : t + 1]
+            codes, scales = w1q[(b, t // 2)]
+            cols = slice((t % 2) * P, (t % 2 + 1) * P)
+            g = col(gain_c, b, t)
+            pb, bent, gbent = {}, {}, {}
             for jh in range(2):
                 js = slice(jh * BANK, (jh + 1) * BANK)
-                pa = ps1.tile([P, BANK], F32, name="pa")
-                pb = ps1.tile([P, BANK], F32, name="pb")
+                pa = ps1.tile([P, BANK], F32, name="pa", bufs=2)
                 nc.tensor.matmul_mx(
-                    out=pa[:], lhsT=w1q[b][0][:, cols].bitcast(FP8X4), lhsT_scale=w1q[b][1][:, cols],
+                    out=pa[:], lhsT=codes[:, cols].bitcast(FP8X4), lhsT_scale=scales[:, cols],
                     rhs=vw[jh][:].bitcast(FP8X4), rhs_scale=vs[:, js], start=True, stop=True,
                 )
+                if jh == 0 and 1 < i:
+                    bent[jh] = hp[:, i - 1, :]
+                else:
+                    bent[jh] = ring.tile([P, BANK], F32, name="bent")[:]
+                nc.scalar.activation(bent[jh], pa[:], ACT.Tanh)
+            for jh in range(2):
+                pb[jh] = ps1.tile([P, BANK], F32, name="pb", bufs=4)
                 nc.tensor.matmul_mx(
-                    out=pb[:], lhsT=w2d[b][:, cols].bitcast(FP8X4),
-                    lhsT_scale=w2scd[:, b * KP + t * P : b * KP + (t + 1) * P],
-                    rhs=vw[jh][:].bitcast(FP8X4), rhs_scale=vs[:, js], start=True, stop=True,
+                    out=pb[jh][:], lhsT=w2d[b][:, 0, t * P : (t + 1) * P].bitcast(FP8X4),
+                    lhsT_scale=w2scd[b][:, 0, t * P : (t + 1) * P],
+                    rhs=vw[jh][:].bitcast(FP8X4), rhs_scale=vs[:, jh * BANK : (jh + 1) * BANK], start=True, stop=True,
                 )
-                bent = ring3.tile([P, BANK], F32, name="bent")
-                nc.scalar.activation(bent[:], pa[:], ACT.Tanh)
-                gbent = ring3.tile([P, BANK], F32, name="gbent")
-                nc.scalar.activation(gbent[:], bent[:], ACT.Copy, scale=g)
-                nc.vector.scalar_tensor_tensor(h[(b, t)][:, js], pb[:], g, gbent[:], MULT, ADD)
-
-        def pick(b, t):
-            nc.vector.tensor_copy(hp[b][:, t, :], h[(b, t)][:].indirect(pos[:]))
+                gbent[jh] = ring.tile([P, BANK], F32, name="gbent", bufs=4)
+                nc.scalar.activation(gbent[jh][:], bent[jh], ACT.Copy, scale=g)
+            if i:
+                pick(i - 1)
+            for jh in range(2):
+                nc.vector.scalar_tensor_tensor(
+                    h[(b, t)][:, jh * BANK : (jh + 1) * BANK], pb[jh][:], g, gbent[jh][:], MULT, ADD
+                )
 
         def second_operands(hf, b):
             walk_out = "p (c i t) -> p c t i"
             walk_in = "p t (c i) -> p c t i"
-            picked = hp[b][:, :, hf * HALF : (hf + 1) * HALF].rearrange(walk_in, i=4)
-            s1 = ring.tile([P, PACK * HALF], BF16, name="s1", align_bytes=64)
+            picked = hp[:, b * PACK : (b + 1) * PACK, hf * HALF : (hf + 1) * HALF].rearrange(walk_in, i=4)
+            s1 = ring.tile([P, PACK * HALF], BF16, name="sx", align_bytes=64, bufs=5)
             nc.scalar.activation(s1[:].rearrange(walk_out, i=4, t=PACK), picked, ACT.Abs)
-            s2 = ring.tile([P, PACK * HALF], BF16, name="s2", align_bytes=64)
-            nc.vector.tensor_tensor(
+            s2 = ring.tile([P, PACK * HALF], BF16, name="sx", align_bytes=64, bufs=5)
+            (nc.gpsimd if (hf, b) in X2G else nc.vector).tensor_tensor(
                 s2[:].rearrange(walk_out, i=4, t=PACK), picked,
                 lap_t[b][:, :, hf * HALF : (hf + 1) * HALF].rearrange(walk_in, i=4), ADD,
             )
@@ -175,79 +212,90 @@ def tile_list_tricot_lapping_inspector_kernel(
         res = {}
 
         def scale_all(b, t):
-            res[(b, t)] = held([P, S], F32, f"res{b}{t}")
-            nc.scalar.activation(res[(b, t)][:], h[(b, t)][:], ACT.Copy, scale=skip_c[:, b, t : t + 1])
+            res[(b, t)] = ring.tile([P, S], F32, name="res", bufs=6)
+            nc.scalar.activation(res[(b, t)][:], h[(b, t)][:], ACT.Copy, scale=col(both_c, b, t))
 
         def second_stage(hf, b, t):
             both = ps2.tile([P, HALF], F32, name="both")
-            c0 = b * KP + t * P
+            cols = slice((t % 2) * P, (t % 2 + 1) * P)
             for a in range(NB):
+                codes, scales = w4q[(a, b, t // 2)]
                 nc.tensor.matmul_mx(
-                    out=both[:], lhsT=w4q[(a, b)][0][:, t * P : (t + 1) * P].bitcast(FP8X4),
-                    lhsT_scale=w4q[(a, b)][1][:, t * P : (t + 1) * P],
+                    out=both[:], lhsT=codes[:, cols].bitcast(FP8X4), lhsT_scale=scales[:, cols],
                     rhs=x2q[(hf, a)][0][:].bitcast(FP8X4), rhs_scale=x2q[(hf, a)][1][:],
                     start=(a == 0), stop=False,
                 )
                 nc.tensor.matmul_mx(
-                    out=both[:], lhsT=w3d[a][:, 2 * c0 : 2 * (c0 + P)].bitcast(FP4X4),
-                    lhsT_scale=w3scd[:, a * H + c0 : a * H + c0 + P],
+                    out=both[:], lhsT=w3d[b][:, a, 2 * t * P : 2 * (t + 1) * P].bitcast(FP4X4),
+                    lhsT_scale=w3scd[b][:, a, t * P : (t + 1) * P],
                     rhs=x1q[(hf, a)][0][:].bitcast(FP8X4), rhs_scale=x1q[(hf, a)][1][:],
                     start=False, stop=(a == NB - 1),
                 )
-            y = ring3.tile([P, HALF], F32, name="y")
-            nc.vector.scalar_tensor_tensor(y[:], both[:], skip_c[:, b, t : t + 1], hp[b][:, t, hf * HALF : (hf + 1) * HALF], MULT, MULT)
-            return y
+            bs = ring3.tile([P, HALF], F32, name="bs", bufs=4)
+            nc.scalar.activation(bs[:], both[:], ACT.Copy, scale=col(skip_c, b, t))
+            return bs
 
-        def put(hf, b, t, y):
+        def put(hf, b, t, bs):
             nc.vector.tensor_tensor(
-                res[(b, t)][:].indirect(pos[:, hf * 16 : (hf + 1) * 16]), y[:],
-                wgo_t[:, t, hf * HALF : (hf + 1) * HALF], MULT,
+                res[(b, t)][:].indirect(pos[:, hf * 16 : (hf + 1) * 16]), bs[:],
+                hw[(b, t)][:, hf * HALF : (hf + 1) * HALF], MULT,
             )
 
+        def w4_pair(b, tp, a):
+            w4q[(a, b, tp)] = weight_pair(nc.scalar.copy, w4_raw[(a, b)], tp, f"w4q{a}{b}{tp}")
+
         tiles = [(b, t) for b in range(NB) for t in range(PACK)]
-        w1q[0] = quantise(round_weight(w1_raw[0], 64), KP, "w1q0")
         vw = []
         for jh in range(2):
             words = held([P, BANK], U32, f"vw{jh}")
             nc.vector.tensor_copy(words[:], tabw[:].indirect(idx[:, jh * 32 : (jh + 1) * 32]))
             vw.append(words)
-            if jh == 0:
-                deal(nc.vector.tensor_copy, w2scd[:], w2sc[:])
-                deal(nc.vector.tensor_copy, w2d[0][:].bitcast(I32), w2w[0][:].bitcast(I32))
+        w1q[(0, 0)] = weight_pair(nc.vector.tensor_copy, w1_raw[0], 0, "w1q00")
+        w1q[(0, 1)] = weight_pair(nc.scalar.copy, w1_raw[0], 1, "w1q01")
+        deal_w2(0, nc.scalar.copy)
         for i, (b, t) in enumerate(tiles):
-            first_stage(b, t)
-            if i > 0:
-                pick(*tiles[i - 1])
-            if i == 1:
-                w1q[1] = quantise(round_weight(w1_raw[1]), KP, "w1q1")
-                deal(nc.vector.tensor_copy, w2d[1][:].bitcast(I32), w2w[1][:].bitcast(I32))
+            first_stage(i)
+            if i == 0:
+                deal_w3s(0)
+                deal_w3s(1)
+            if i == 2:
+                w1q[(1, 0)] = weight_pair(nc.vector.tensor_copy, w1_raw[1], 0, "w1q10")
+                deal_w2(1, nc.vector.tensor_copy)
             if i == 4:
-                w4q[(0, 0)] = quantise(round_weight(w4_raw[(0, 0)]), KP, "w4q00")
-            if i == 5:
-                second_operands(0, 0)
-            if i == 6:
-                w4q[(1, 0)] = quantise(round_weight(w4_raw[(1, 0)]), KP, "w4q10")
-        pick(*tiles[-1])
+                w1q[(1, 1)] = weight_pair(nc.scalar.copy, w1_raw[1], 1, "w1q11")
+        pick(len(tiles) - 1)
+        w4_pair(0, 0, 0)
+        w4_pair(0, 0, 1)
+        second_operands(0, 0)
+        deal_w3(0)
+        scale_all(0, 0)
         second_operands(0, 1)
-        deal(nc.vector.tensor_copy, w3scd[:], w3sc[:].rearrange("p a c -> p (a c)"))
-        for a in range(NB):
-            deal(nc.scalar.copy, w3d[a][:].bitcast(U16), w3w[a][:].bitcast(U16))
 
         out_rows = out.rearrange("(b p t) j -> b t p j", b=NB, t=PACK)
-        steps = [(hf, b, t) for hf in range(2) for (b, t) in tiles]
+        steps = [(hf, b, t) for b in range(NB) for hf in range(2) for t in range(PACK)]
         ys = {}
         for n, (hf, b, t) in enumerate(steps):
-            if hf == 0:
-                scale_all(b, t)
             ys[n] = second_stage(hf, b, t)
             if n == 0:
-                second_operands(1, 0)
+                w4_pair(0, 1, 0)
+                w4_pair(0, 1, 1)
+            if n < 3:
+                scale_all(0, n + 1)
             if n == 1:
-                w4q[(0, 1)] = quantise(round_weight(w4_raw[(0, 1)]), KP, "w4q01")
+                second_operands(1, 0)
             if n == 2:
-                w4q[(1, 1)] = quantise(round_weight(w4_raw[(1, 1)]), KP, "w4q11")
-            if n == 4:
                 second_operands(1, 1)
+            if n == 3:
+                w4_pair(1, 0, 0)
+                w4_pair(1, 0, 1)
+            if n == 4:
+                deal_w3(1)
+            if n == 5:
+                w4_pair(1, 1, 0)
+            if n == 6:
+                w4_pair(1, 1, 1)
+            if 6 <= n < 10:
+                scale_all(1, n - 6)
             if n > 0:
                 put(*steps[n - 1], ys[n - 1])
                 if steps[n - 1][0] == 1:

@@ -36,7 +36,7 @@ def tile_list_tricot_lapping_inspector_kernel(
     nc = tc.nc
     with ExitStack() as ctx:
         keep = ctx.enter_context(tc.tile_pool(name="keep", bufs=1))
-        raw = ctx.enter_context(tc.tile_pool(name="raw", bufs=3))
+        raw = ctx.enter_context(tc.tile_pool(name="raw", bufs=4))
         ring = ctx.enter_context(tc.tile_pool(name="ring", bufs=2))
         ring3 = ctx.enter_context(tc.tile_pool(name="ring3", bufs=3))
         ps1 = ctx.enter_context(tc.psum_pool(name="ps1", bufs=3))
@@ -110,8 +110,8 @@ def tile_list_tricot_lapping_inspector_kernel(
         vs = held([P, S], U8, "vs")
         nc.vector.tensor_copy(vs[:], tabs[:].indirect(idx[:]))
 
-        def deal(move, dst, src):
-            move(dst.rearrange("p a (t m) -> p a m t", t=PACK), src.rearrange("p a (m t) -> p a m t", t=PACK))
+        def deal(move, dst, src, walk="p a t m"):
+            move(dst.rearrange("p a (t m) -> " + walk, t=PACK), src.rearrange("p a (m t) -> " + walk, t=PACK))
 
         def quantise(staged, width, name):
             codes = held([P, width], U32, name + "c")
@@ -134,7 +134,7 @@ def tile_list_tricot_lapping_inspector_kernel(
 
         def deal_w2(b, move):
             deal(nc.vector.tensor_copy, w2scd[b][:], w2sc[:, b * KP : (b + 1) * KP].rearrange("p (a c) -> p a c", a=1))
-            deal(move, w2d[b][:], w2w[b][:].rearrange("p (a c) -> p a c", a=1))
+            deal(move, w2d[b][:], w2w[b][:].rearrange("p (a c) -> p a c", a=1), "p a m t")
 
         def deal_w3s(b):
             deal(movers[W3S], w3scd[b][:], w3sc[:, :, b * KP : (b + 1) * KP])
@@ -145,7 +145,9 @@ def tile_list_tricot_lapping_inspector_kernel(
         h = {}
         hp = held([P, NB * PACK, NP], F32, "hp")
         hw = {}
-        w1q, w4q, x1q, x2q = {}, {}, {}, {}
+        w1q, w4q = {}, {}
+        x1q = [(held([P, NP], U32, f"x1c{b}"), held([P, NP], U8, f"x1s{b}")) for b in range(NB)]
+        x2q = [(held([P, NP], U32, f"x2c{b}"), held([P, NP], U8, f"x2s{b}")) for b in range(NB)]
         both_c = skip_c
         if UWIN:
             both_c = held([P, NB * PACK], F32, "both_c")
@@ -154,11 +156,16 @@ def tile_list_tricot_lapping_inspector_kernel(
         def col(cols, b, t):
             return cols[:, b * PACK + t : b * PACK + t + 1]
 
+        def weigh(eng, i):
+            b, t = tiles[i]
+            eng.tensor_tensor(hw[(b, t)][:], hp[:, i, :], wgo_t[:, t, :], MULT)
+
         def pick(i):
             b, t = tiles[i]
             nc.vector.tensor_copy(hp[:, i, :], h[(b, t)][:].indirect(pos[:]))
             hw[(b, t)] = held([P, NP], F32, f"hw{b}{t}")
-            nc.gpsimd.tensor_tensor(hw[(b, t)][:], hp[:, i, :], wgo_t[:, t, :], MULT)
+            if i < 7:
+                weigh(nc.gpsimd, i)
 
         def first_stage(i):
             b, t = tiles[i]
@@ -198,47 +205,48 @@ def tile_list_tricot_lapping_inspector_kernel(
         def second_operands(hf, b):
             walk_out = "p (c i t) -> p c t i"
             walk_in = "p t (c i) -> p c t i"
-            picked = hp[:, b * PACK : (b + 1) * PACK, hf * HALF : (hf + 1) * HALF].rearrange(walk_in, i=4)
+            picked = hp[:, b * PACK : (b + 1) * PACK, hf * HALF : (hf + 1) * HALF].rearrange(walk_in, i=2)
             s1 = ring.tile([P, PACK * HALF], BF16, name="sx", align_bytes=64, bufs=5)
-            nc.scalar.activation(s1[:].rearrange(walk_out, i=4, t=PACK), picked, ACT.Abs)
+            nc.scalar.activation(s1[:].rearrange(walk_out, i=2, t=PACK), picked, ACT.Abs)
             s2 = ring.tile([P, PACK * HALF], BF16, name="sx", align_bytes=64, bufs=5)
             (nc.gpsimd if (hf, b) in X2G else nc.vector).tensor_tensor(
-                s2[:].rearrange(walk_out, i=4, t=PACK), picked,
-                lap_t[b][:, :, hf * HALF : (hf + 1) * HALF].rearrange(walk_in, i=4), ADD,
+                s2[:].rearrange(walk_out, i=2, t=PACK), picked,
+                lap_t[b][:, :, hf * HALF : (hf + 1) * HALF].rearrange(walk_in, i=2), ADD,
             )
-            x2q[(hf, b)] = quantise(s2, HALF, f"x2{hf}{b}")
-            x1q[(hf, b)] = quantise(s1, HALF, f"x1{hf}{b}")
+            ms = slice(hf * HALF, (hf + 1) * HALF)
+            nc.vector.quantize_mx(out=x2q[b][0][:, ms].bitcast(FP8X4), scales=x2q[b][1][:, ms], in_=s2[:])
+            nc.vector.quantize_mx(out=x1q[b][0][:, ms].bitcast(FP8X4), scales=x1q[b][1][:, ms], in_=s1[:])
 
         res = {}
 
         def scale_all(b, t):
-            res[(b, t)] = ring.tile([P, S], F32, name="res", bufs=6)
+            res[(b, t)] = ring.tile([P, S], F32, name="res", bufs=4)
             nc.scalar.activation(res[(b, t)][:], h[(b, t)][:], ACT.Copy, scale=col(both_c, b, t))
 
-        def second_stage(hf, b, t):
-            both = ps2.tile([P, HALF], F32, name="both")
+        def second_stage(m0, m1, b, t):
+            both = ps2.tile([P, m1 - m0], F32, name="both")
             cols = slice((t % 2) * P, (t % 2 + 1) * P)
             for a in range(NB):
                 codes, scales = w4q[(a, b, t // 2)]
                 nc.tensor.matmul_mx(
                     out=both[:], lhsT=codes[:, cols].bitcast(FP8X4), lhsT_scale=scales[:, cols],
-                    rhs=x2q[(hf, a)][0][:].bitcast(FP8X4), rhs_scale=x2q[(hf, a)][1][:],
+                    rhs=x2q[a][0][:, m0:m1].bitcast(FP8X4), rhs_scale=x2q[a][1][:, m0:m1],
                     start=(a == 0), stop=False,
                 )
                 nc.tensor.matmul_mx(
                     out=both[:], lhsT=w3d[b][:, a, 2 * t * P : 2 * (t + 1) * P].bitcast(FP4X4),
                     lhsT_scale=w3scd[b][:, a, t * P : (t + 1) * P],
-                    rhs=x1q[(hf, a)][0][:].bitcast(FP8X4), rhs_scale=x1q[(hf, a)][1][:],
+                    rhs=x1q[a][0][:, m0:m1].bitcast(FP8X4), rhs_scale=x1q[a][1][:, m0:m1],
                     start=False, stop=(a == NB - 1),
                 )
-            bs = ring3.tile([P, HALF], F32, name="bs", bufs=4)
+            bs = ring3.tile([P, m1 - m0], F32, name="bs", bufs=3)
             nc.scalar.activation(bs[:], both[:], ACT.Copy, scale=col(skip_c, b, t))
             return bs
 
-        def put(hf, b, t, bs):
+        def put(m0, m1, b, t, bs):
             nc.vector.tensor_tensor(
-                res[(b, t)][:].indirect(pos[:, hf * 16 : (hf + 1) * 16]), bs[:],
-                hw[(b, t)][:, hf * HALF : (hf + 1) * HALF], MULT,
+                res[(b, t)][:].indirect(pos[:, m0 // 16 : m1 // 16]), bs[:],
+                hw[(b, t)][:, m0:m1], MULT,
             )
 
         def w4_pair(b, tp, a):
@@ -263,42 +271,47 @@ def tile_list_tricot_lapping_inspector_kernel(
                 deal_w2(1, nc.vector.tensor_copy)
             if i == 4:
                 w1q[(1, 1)] = weight_pair(nc.scalar.copy, w1_raw[1], 1, "w1q11")
+            if i == 4:
+                scale_all(0, 0)
         pick(len(tiles) - 1)
         w4_pair(0, 0, 0)
         w4_pair(0, 0, 1)
         second_operands(0, 0)
         deal_w3(0)
-        scale_all(0, 0)
+        scale_all(0, 1)
         second_operands(0, 1)
 
+
         out_rows = out.rearrange("(b p t) j -> b t p j", b=NB, t=PACK)
-        steps = [(hf, b, t) for b in range(NB) for hf in range(2) for t in range(PACK)]
+        steps = [(hf * HALF, (hf + 1) * HALF, 0, t) for hf in range(2) for t in range(2)]
+        steps += [(0, NP, b, t) for b, t in tiles[2:]]
         ys = {}
-        for n, (hf, b, t) in enumerate(steps):
-            ys[n] = second_stage(hf, b, t)
+        for n, (m0, m1, b, t) in enumerate(steps):
+            ys[n] = second_stage(m0, m1, b, t)
             if n == 0:
+                second_operands(1, 0)
+            if n == 1:
+                second_operands(1, 1)
+                weigh(nc.vector, 7)
+            if n == 2:
                 w4_pair(0, 1, 0)
                 w4_pair(0, 1, 1)
-            if n < 3:
-                scale_all(0, n + 1)
-            if n == 1:
-                second_operands(1, 0)
-            if n == 2:
-                second_operands(1, 1)
             if n == 3:
+                scale_all(0, 2)
+            if n == 4:
+                scale_all(0, 3)
                 w4_pair(1, 0, 0)
                 w4_pair(1, 0, 1)
-            if n == 4:
-                deal_w3(1)
             if n == 5:
-                w4_pair(1, 1, 0)
+                deal_w3(1)
             if n == 6:
+                w4_pair(1, 1, 0)
                 w4_pair(1, 1, 1)
-            if 6 <= n < 10:
-                scale_all(1, n - 6)
+            if 5 <= n < 9:
+                scale_all(1, n - 5)
             if n > 0:
                 put(*steps[n - 1], ys[n - 1])
-                if steps[n - 1][0] == 1:
-                    nc.sync.dma_start(out_rows[steps[n - 1][1], steps[n - 1][2]], res[steps[n - 1][1:]][:])
+                if steps[n - 1][1] == NP:
+                    nc.sync.dma_start(out_rows[steps[n - 1][2], steps[n - 1][3]], res[steps[n - 1][2:]][:])
         put(*steps[-1], ys[len(steps) - 1])
-        nc.sync.dma_start(out_rows[steps[-1][1], steps[-1][2]], res[steps[-1][1:]][:])
+        nc.sync.dma_start(out_rows[steps[-1][2], steps[-1][3]], res[steps[-1][2:]][:])

@@ -24,10 +24,10 @@ NB = H // KP
 BANK = 512
 HALF = NP // 2
 PAIR = 2 * P
-UWIN = False
-X2G = ()
-W3W = "S"
-W3S = "V"
+PER_COL = 16
+QUADS = 4
+ROW_TILES = [(b, t) for b in range(NB) for t in range(PACK)]
+LAST = len(ROW_TILES) - 1
 
 
 def tile_list_tricot_lapping_inspector_kernel(
@@ -41,31 +41,30 @@ def tile_list_tricot_lapping_inspector_kernel(
         ring3 = ctx.enter_context(tc.tile_pool(name="ring3", bufs=3))
         ps1 = ctx.enter_context(tc.psum_pool(name="ps1", bufs=3))
         ps2 = ctx.enter_context(tc.psum_pool(name="ps2", bufs=2))
-        movers = {"S": nc.scalar.copy, "V": nc.vector.tensor_copy, "G": nc.gpsimd.tensor_copy}
 
         def held(shape, dtype, name):
             return keep.tile(shape, dtype, name=name, align_bytes=64)
 
-        idx = held([P, S // 16], U16, "idx")
-        pos = held([P, NP // 16], U16, "pos")
-        tabw = held([P, T], U32, "tabw")
-        tabs = held([P, T], U8, "tabs")
-        w2sc = held([P, H], U8, "w2sc")
-        w3sc = held([P, NB, H], U8, "w3sc")
-        w2w = [held([P, KP], U32, f"w2w{b}") for b in range(NB)]
-        w3w = held([P, NB, 2 * H], U8, "w3w")
+        idx = held([P, S // PER_COL], U16, "idx")
+        pos = held([P, NP // PER_COL], U16, "pos")
+        tab_w = held([P, T], U32, "tab_w")
+        tab_s = held([P, T], U8, "tab_s")
+        w2_s = held([P, H], U8, "w2_s")
+        w3_s = held([P, NB, H], U8, "w3_s")
+        w2_w = [held([P, KP], U32, f"w2_w{b}") for b in range(NB)]
+        w3_w = [held([P, NB, 2 * KP], U8, f"w3_w{b}") for b in range(NB)]
         gain_c = held([P, NB * PACK], F32, "gain_c")
         skip_c = held([P, NB * PACK], F32, "skip_c")
-        lap_t = [held([P, PACK, NP], F32, f"lap{b}") for b in range(NB)]
-        wgo_t = held([P, PACK, NP], F32, "wgo_t")
+        lap_t = {(hf, b): held([P, PACK, HALF], F32, f"lap{hf}{b}") for hf in range(2) for b in range(NB)}
+        wgo_t = [held([P, 2, NP], F32, f"wgo{tp}") for tp in range(2)]
 
-        nc.gpsimd.memset(tabs[:].bitcast(I32), 0)
-        nc.gpsimd.memset(w2sc[:].bitcast(I32), 0)
-        nc.gpsimd.memset(w3sc[:].rearrange("p a c -> p (a c)").bitcast(I32), 0)
+        nc.gpsimd.memset(tab_s[:].bitcast(I32), 0)
+        nc.gpsimd.memset(w2_s[:].bitcast(I32), 0)
+        nc.gpsimd.memset(w3_s[:].rearrange("p a c -> p (a c)").bitcast(I32), 0)
 
-        def load_scale_rows(plane, rows, quads):
+        def load_scale_rows(dst, rows, quads):
             for q in quads:
-                nc.sync.dma_start(plane[32 * q : 32 * q + 4, :].bitcast(I32), rows[4 * q : 4 * q + 4, :].bitcast(I32))
+                nc.sync.dma_start(dst[32 * q : 32 * q + 4, :].bitcast(I32), rows[4 * q : 4 * q + 4, :].bitcast(I32))
 
         def load_weight(w, a, b):
             piece = raw.tile([P, PACK, KP], F32, name="piece")
@@ -74,44 +73,60 @@ def tile_list_tricot_lapping_inspector_kernel(
             )
             return piece
 
-        def load_rows(cols, vec):
+        def load_per_row(cols, vec):
             nc.sync.dma_start(
                 cols[:].rearrange("p (b t) -> p b t", b=NB), vec.rearrange("(b p t) -> p b t", b=NB, t=PACK)
             )
 
-        w2_all = w2_words[0].rearrange("p c i -> p (c i)")
+        def load_w2(b):
+            words = w2_words[0].rearrange("p c i -> p (c i)")[:, PACK * b * KP : PACK * (b + 1) * KP]
+            nc.sync.dma_start(w2_w[b][:].bitcast(I32), words.bitcast(I32))
+
+        def load_w3(b):
+            words = w3_words[:, :, 2 * b * KP : 2 * (b + 1) * KP].rearrange("a p c -> p a c")
+            nc.sync.dma_start(w3_w[b][:].bitcast(I32), words.bitcast(I32))
+
+        def load_lap(hf, b):
+            rows = lap[b * KP : (b + 1) * KP, hf * HALF : (hf + 1) * HALF]
+            nc.sync.dma_start(lap_t[(hf, b)][:], rows.rearrange("(p t) m -> p t m", t=PACK))
+
+        def load_wgo(tp):
+            for q in (0, 2, 1, 3):
+                nc.sync.dma_start(
+                    wgo_t[tp][32 * q : 32 * q + 32], wgo.rearrange("(p t) m -> p t m", t=PACK)[:, 2 * tp : 2 * tp + 2]
+                )
 
         nc.sync.dma_start(idx[:], offs)
         nc.sync.dma_start(pos[:], pos1)
-        load_scale_rows(tabs, tab_scales[0], range(4))
-        nc.sync.dma_start(tabw[:].bitcast(I32), tab_words[0].rearrange("p c i -> p (c i)").bitcast(I32))
-        load_scale_rows(w2sc, w2_scales[0], range(1))
+        load_scale_rows(tab_s, tab_scales[0], range(QUADS))
+        nc.sync.dma_start(tab_w[:].bitcast(I32), tab_words[0].rearrange("p c i -> p (c i)").bitcast(I32))
+        load_scale_rows(w2_s, w2_scales[0], range(1))
         w1_raw = [load_weight(w1, 0, 0)]
-        nc.sync.dma_start(w2w[0][:].bitcast(I32), w2_all[:, 0 : 4 * KP].bitcast(I32))
-        load_scale_rows(w2sc, w2_scales[0], range(1, 4))
-        load_rows(gain_c, gain)
-        for q in range(4):
-            (nc.gpsimd if q > 1 else nc.sync).dma_start(
-                w3sc[32 * q : 32 * q + 4].bitcast(I32),
+        load_w2(0)
+        load_scale_rows(w2_s, w2_scales[0], range(1, QUADS))
+        load_per_row(gain_c, gain)
+        for q in range(QUADS):
+            (nc.sync if q < QUADS // 2 else nc.gpsimd).dma_start(
+                w3_s[32 * q : 32 * q + 4].bitcast(I32),
                 w3_scales[:, 4 * q : 4 * q + 4, :].rearrange("a q c -> q a c").bitcast(I32),
             )
         w1_raw.append(load_weight(w1, 0, 1))
-        for q in range(4):
-            nc.sync.dma_start(wgo_t[32 * q : 32 * q + 32], wgo.rearrange("(p t) m -> p t m", t=PACK))
-        nc.sync.dma_start(w2w[1][:].bitcast(I32), w2_all[:, 4 * KP : 8 * KP].bitcast(I32))
-        load_rows(skip_c, skip)
-        nc.sync.dma_start(lap_t[0][:], lap[0:KP, :].rearrange("(p t) m -> p t m", t=PACK))
+        load_w2(1)
+        load_wgo(0)
+        load_per_row(skip_c, skip)
+        load_wgo(1)
+        load_lap(0, 0)
         w4_raw = {(a, 0): load_weight(w4, a, 0) for a in range(NB)}
-        nc.sync.dma_start(w3w[:].bitcast(I32), w3_words.rearrange("a p c -> p a c").bitcast(I32))
-        nc.sync.dma_start(lap_t[1][:], lap[KP : 2 * KP, :].rearrange("(p t) m -> p t m", t=PACK))
+        load_lap(0, 1)
+        load_w3(0)
+        for b in range(NB):
+            load_lap(1, b)
         for a in range(NB):
             w4_raw[(a, 1)] = load_weight(w4, a, 1)
+        load_w3(1)
 
-        vs = held([P, S], U8, "vs")
-        nc.vector.tensor_copy(vs[:], tabs[:].indirect(idx[:]))
-
-        def deal(move, dst, src, walk="p a t m"):
-            move(dst.rearrange("p a (t m) -> " + walk, t=PACK), src.rearrange("p a (m t) -> " + walk, t=PACK))
+        def deal(move, dst, src, walk):
+            move(dst.rearrange("q a (t p) -> " + walk, t=PACK), src.rearrange("q a (p t) -> " + walk, t=PACK))
 
         def quantise(staged, width, name):
             codes = held([P, width], U32, name + "c")
@@ -119,199 +134,226 @@ def tile_list_tricot_lapping_inspector_kernel(
             nc.vector.quantize_mx(out=codes[:].bitcast(FP8X4), scales=scales[:], in_=staged[:])
             return codes, scales
 
-        def weight_pair(move, piece, tp, name):
+        def round_pair(move, piece, tp):
             staged = ring.tile([P, PACK * PAIR], BF16, name="staged", align_bytes=64, bufs=3)
             move(
-                staged[:].rearrange("p (t m j) -> p m j t", t=2, j=PACK),
-                piece[:].rearrange("p j (m t) -> p m j t", t=PACK)[:, :, :, 2 * tp : 2 * tp + 2],
+                staged[:].rearrange("q (t p j) -> q p j t", t=2, j=PACK),
+                piece[:].rearrange("q j (p t) -> q p j t", t=PACK)[:, :, :, 2 * tp : 2 * tp + 2],
             )
-            return quantise(staged, PAIR, name)
+            return staged
 
-        w2scd = [held([P, 1, KP], U8, f"w2scd{b}") for b in range(NB)]
-        w2d = [held([P, 1, KP], U32, f"w2d{b}") for b in range(NB)]
-        w3scd = [held([P, NB, KP], U8, f"w3scd{b}") for b in range(NB)]
-        w3d = [held([P, NB, 2 * KP], U8, f"w3d{b}") for b in range(NB)]
-
-        def deal_w2(b, move):
-            deal(nc.vector.tensor_copy, w2scd[b][:], w2sc[:, b * KP : (b + 1) * KP].rearrange("p (a c) -> p a c", a=1))
-            deal(move, w2d[b][:], w2w[b][:].rearrange("p (a c) -> p a c", a=1), "p a m t")
-
-        def deal_w3s(b):
-            deal(movers[W3S], w3scd[b][:], w3sc[:, :, b * KP : (b + 1) * KP])
-
-        def deal_w3(b):
-            deal(movers[W3W], w3d[b][:].bitcast(U16), w3w[:, :, 2 * b * KP : 2 * (b + 1) * KP].bitcast(U16))
-
-        h = {}
-        hp = held([P, NB * PACK, NP], F32, "hp")
-        hw = {}
+        w2_sd = [held([P, 1, KP], U8, f"w2_sd{b}") for b in range(NB)]
+        w2_wd = [held([P, 1, KP], U32, f"w2_wd{b}") for b in range(NB)]
+        w3_sd = [held([P, NB, KP], U8, f"w3_sd{b}") for b in range(NB)]
+        w3_wd = [held([P, NB, 2 * KP], U8, f"w3_wd{b}") for b in range(NB)]
         w1q, w4q = {}, {}
-        x1q = [(held([P, NP], U32, f"x1c{b}"), held([P, NP], U8, f"x1s{b}")) for b in range(NB)]
-        x2q = [(held([P, NP], U32, f"x2c{b}"), held([P, NP], U8, f"x2s{b}")) for b in range(NB)]
-        both_c = skip_c
-        if UWIN:
-            both_c = held([P, NB * PACK], F32, "both_c")
-            nc.vector.tensor_tensor(both_c[:], gain_c[:], skip_c[:], MULT)
+
+        def deal_w2(b, move_words):
+            scale_bytes = w2_s[:, b * KP : (b + 1) * KP].rearrange("q (a c) -> q a c", a=1)
+            deal(nc.vector.tensor_copy, w2_sd[b][:], scale_bytes, "q a t p")
+            deal(move_words, w2_wd[b][:], w2_w[b][:].rearrange("q (a c) -> q a c", a=1), "q a p t")
+
+        def deal_w3_scales(b):
+            deal(nc.vector.tensor_copy, w3_sd[b][:], w3_s[:, :, b * KP : (b + 1) * KP], "q a t p")
+
+        def deal_w3_words(b):
+            deal(nc.scalar.copy, w3_wd[b][:].bitcast(U16), w3_w[b][:].bitcast(U16), "q a t p")
+
+        def w1_pair(move, b, tp):
+            w1q[(b, tp)] = quantise(round_pair(move, w1_raw[b], tp), PAIR, f"w1q{b}{tp}")
+
+        def w4_round(a, b, tp):
+            return round_pair(nc.scalar.copy, w4_raw[(a, b)], tp)
+
+        def w4_quantise(a, b, tp, staged):
+            w4q[(a, b, tp)] = quantise(staged, PAIR, f"w4q{a}{b}{tp}")
+
+        def w4_pair(b, tp):
+            for a in range(NB):
+                w4_quantise(a, b, tp, w4_round(a, b, tp))
 
         def col(cols, b, t):
             return cols[:, b * PACK + t : b * PACK + t + 1]
 
-        def weigh(eng, i):
-            b, t = tiles[i]
-            eng.tensor_tensor(hw[(b, t)][:], hp[:, i, :], wgo_t[:, t, :], MULT)
+        h = {}
+        hp = [held([P, PACK, NP], F32, f"hp{b}") for b in range(NB)]
+        hw = {}
+
+        def weigh(engine, i, where):
+            b, t = ROW_TILES[i]
+            hw[(b, t)] = where
+            engine.tensor_tensor(where, hp[b][:, t, :], wgo_t[t // 2][:, t % 2, :], MULT)
 
         def pick(i):
-            b, t = tiles[i]
-            nc.vector.tensor_copy(hp[:, i, :], h[(b, t)][:].indirect(pos[:]))
-            hw[(b, t)] = held([P, NP], F32, f"hw{b}{t}")
-            if i < 7:
-                weigh(nc.gpsimd, i)
+            b, t = ROW_TILES[i]
+            nc.vector.tensor_copy(hp[b][:, t, :], h[(b, t)][:].indirect(pos[:]))
 
         def first_stage(i):
-            b, t = tiles[i]
+            b, t = ROW_TILES[i]
             h[(b, t)] = held([P, S], F32, f"h{b}{t}")
             codes, scales = w1q[(b, t // 2)]
             cols = slice((t % 2) * P, (t % 2 + 1) * P)
             g = col(gain_c, b, t)
-            pb, bent, gbent = {}, {}, {}
-            for jh in range(2):
-                js = slice(jh * BANK, (jh + 1) * BANK)
-                pa = ps1.tile([P, BANK], F32, name="pa", bufs=2)
+            halves = [slice(jh * BANK, (jh + 1) * BANK) for jh in range(2)]
+            bent, straight, gbent = [], [], []
+            for jh, js in enumerate(halves):
+                curve = ps1.tile([P, BANK], F32, name="curve", bufs=2)
                 nc.tensor.matmul_mx(
-                    out=pa[:], lhsT=codes[:, cols].bitcast(FP8X4), lhsT_scale=scales[:, cols],
-                    rhs=vw[jh][:].bitcast(FP8X4), rhs_scale=vs[:, js], start=True, stop=True,
+                    out=curve[:], lhsT=codes[:, cols].bitcast(FP8X4), lhsT_scale=scales[:, cols],
+                    rhs=v_w[jh][:].bitcast(FP8X4), rhs_scale=v_s[:, js], start=True, stop=True,
                 )
-                if jh == 0 and 1 < i:
-                    bent[jh] = hp[:, i - 1, :]
+                if jh == 0 and i >= 2:
+                    bent.append(hp[(i - 1) // PACK][:, (i - 1) % PACK, :])
                 else:
-                    bent[jh] = ring.tile([P, BANK], F32, name="bent")[:]
-                nc.scalar.activation(bent[jh], pa[:], ACT.Tanh)
-            for jh in range(2):
-                pb[jh] = ps1.tile([P, BANK], F32, name="pb", bufs=4)
+                    bent.append(ring.tile([P, BANK], F32, name="bent")[:])
+                nc.scalar.activation(bent[jh], curve[:], ACT.Tanh)
+            for jh, js in enumerate(halves):
+                straight.append(ps1.tile([P, BANK], F32, name="straight", bufs=4))
                 nc.tensor.matmul_mx(
-                    out=pb[jh][:], lhsT=w2d[b][:, 0, t * P : (t + 1) * P].bitcast(FP8X4),
-                    lhsT_scale=w2scd[b][:, 0, t * P : (t + 1) * P],
-                    rhs=vw[jh][:].bitcast(FP8X4), rhs_scale=vs[:, jh * BANK : (jh + 1) * BANK], start=True, stop=True,
+                    out=straight[jh][:], lhsT=w2_wd[b][:, 0, t * P : (t + 1) * P].bitcast(FP8X4),
+                    lhsT_scale=w2_sd[b][:, 0, t * P : (t + 1) * P],
+                    rhs=v_w[jh][:].bitcast(FP8X4), rhs_scale=v_s[:, js], start=True, stop=True,
                 )
-                gbent[jh] = ring.tile([P, BANK], F32, name="gbent", bufs=4)
+                gbent.append(ring.tile([P, BANK], F32, name="gbent", bufs=4))
                 nc.scalar.activation(gbent[jh][:], bent[jh], ACT.Copy, scale=g)
-            if i:
+            if i >= 1:
                 pick(i - 1)
-            for jh in range(2):
-                nc.vector.scalar_tensor_tensor(
-                    h[(b, t)][:, jh * BANK : (jh + 1) * BANK], pb[jh][:], g, gbent[jh][:], MULT, ADD
-                )
+                weigh(nc.gpsimd, i - 1, held([P, NP], F32, f"hw{i - 1}")[:])
+            for jh, js in enumerate(halves):
+                nc.vector.scalar_tensor_tensor(h[(b, t)][:, js], straight[jh][:], g, gbent[jh][:], MULT, ADD)
 
-        def second_operands(hf, b):
-            walk_out = "p (c i t) -> p c t i"
-            walk_in = "p t (c i) -> p c t i"
-            picked = hp[:, b * PACK : (b + 1) * PACK, hf * HALF : (hf + 1) * HALF].rearrange(walk_in, i=2)
-            s1 = ring.tile([P, PACK * HALF], BF16, name="sx", align_bytes=64, bufs=5)
-            nc.scalar.activation(s1[:].rearrange(walk_out, i=2, t=PACK), picked, ACT.Abs)
-            s2 = ring.tile([P, PACK * HALF], BF16, name="sx", align_bytes=64, bufs=5)
-            (nc.gpsimd if (hf, b) in X2G else nc.vector).tensor_tensor(
-                s2[:].rearrange(walk_out, i=2, t=PACK), picked,
-                lap_t[b][:, :, hf * HALF : (hf + 1) * HALF].rearrange(walk_in, i=2), ADD,
-            )
-            ms = slice(hf * HALF, (hf + 1) * HALF)
-            nc.vector.quantize_mx(out=x2q[b][0][:, ms].bitcast(FP8X4), scales=x2q[b][1][:, ms], in_=s2[:])
-            nc.vector.quantize_mx(out=x1q[b][0][:, ms].bitcast(FP8X4), scales=x1q[b][1][:, ms], in_=s1[:])
+        width = PACK * HALF
+        plain = [held([P, width], BF16, f"stage{n}")[:] for n in range(4)]
+        wide = held([P, 2 * width], BF16, "wide")
+        stage = {
+            ("size", 0, 0): plain[0],
+            ("shift", 0, 0): plain[1],
+            ("size", 0, 1): wide[:, width // 2 : width // 2 + width],
+            ("shift", 0, 1): plain[2],
+            ("size", 1, 0): plain[3],
+            ("shift", 1, 0): wide[:, :width],
+            ("size", 1, 1): plain[1],
+            ("shift", 1, 1): wide[:, width:],
+        }
+        xq = {}
+        read_walk, write_walk = "p t (c i) -> p c t i", "p (c i t) -> p c t i"
+
+        def picked(hf, b):
+            return hp[b][:, :, hf * HALF : (hf + 1) * HALF].rearrange(read_walk, i=2)
+
+        def make_size(hf, b):
+            nc.scalar.activation(stage[("size", hf, b)].rearrange(write_walk, i=2, t=PACK), picked(hf, b), ACT.Abs)
+
+        def make_shift(hf, b):
+            laps = lap_t[(hf, b)][:].rearrange(read_walk, i=2)
+            woven = stage[("shift", hf, b)].rearrange(write_walk, i=2, t=PACK)
+            nc.vector.tensor_tensor(woven, picked(hf, b), laps, ADD)
+
+        def x_quantise(kind, hf, b):
+            xq[(kind, hf, b)] = quantise(stage[(kind, hf, b)], HALF, f"{kind}{hf}{b}")
 
         res = {}
+        out_rows = out.rearrange("(b p t) j -> b t p j", b=NB, t=PACK)
 
-        def scale_all(b, t):
+        def scale_all(i):
+            b, t = ROW_TILES[i]
             res[(b, t)] = ring.tile([P, S], F32, name="res", bufs=4)
-            nc.scalar.activation(res[(b, t)][:], h[(b, t)][:], ACT.Copy, scale=col(both_c, b, t))
+            nc.scalar.activation(res[(b, t)][:], h[(b, t)][:], ACT.Copy, scale=col(skip_c, b, t))
 
         def second_stage(m0, m1, b, t):
             both = ps2.tile([P, m1 - m0], F32, name="both")
             cols = slice((t % 2) * P, (t % 2 + 1) * P)
-            for a in range(NB):
-                codes, scales = w4q[(a, b, t // 2)]
-                nc.tensor.matmul_mx(
-                    out=both[:], lhsT=codes[:, cols].bitcast(FP8X4), lhsT_scale=scales[:, cols],
-                    rhs=x2q[a][0][:, m0:m1].bitcast(FP8X4), rhs_scale=x2q[a][1][:, m0:m1],
-                    start=(a == 0), stop=False,
-                )
-                nc.tensor.matmul_mx(
-                    out=both[:], lhsT=w3d[b][:, a, 2 * t * P : 2 * (t + 1) * P].bitcast(FP4X4),
-                    lhsT_scale=w3scd[b][:, a, t * P : (t + 1) * P],
-                    rhs=x1q[a][0][:, m0:m1].bitcast(FP8X4), rhs_scale=x1q[a][1][:, m0:m1],
-                    start=False, stop=(a == NB - 1),
-                )
-            bs = ring3.tile([P, m1 - m0], F32, name="bs", bufs=3)
-            nc.scalar.activation(bs[:], both[:], ACT.Copy, scale=col(skip_c, b, t))
-            return bs
+            for hf in range(m0 // HALF, m1 // HALF):
+                ms = slice(hf * HALF - m0, (hf + 1) * HALF - m0)
+                for a in range(NB):
+                    codes, scales = w4q[(a, b, t // 2)]
+                    shift, size = xq[("shift", hf, a)], xq[("size", hf, a)]
+                    nc.tensor.matmul_mx(
+                        out=both[:, ms], lhsT=codes[:, cols].bitcast(FP8X4), lhsT_scale=scales[:, cols],
+                        rhs=shift[0][:].bitcast(FP8X4), rhs_scale=shift[1][:], start=(a == 0), stop=False,
+                    )
+                    nc.tensor.matmul_mx(
+                        out=both[:, ms], lhsT=w3_wd[b][:, a, 2 * t * P : 2 * (t + 1) * P].bitcast(FP4X4),
+                        lhsT_scale=w3_sd[b][:, a, t * P : (t + 1) * P],
+                        rhs=size[0][:].bitcast(FP8X4), rhs_scale=size[1][:], start=False, stop=(a == NB - 1),
+                    )
+            scaled = ring3.tile([P, m1 - m0], F32, name="scaled")
+            nc.scalar.activation(scaled[:], both[:], ACT.Copy, scale=col(skip_c, b, t))
+            return scaled
 
-        def put(m0, m1, b, t, bs):
-            nc.vector.tensor_tensor(
-                res[(b, t)][:].indirect(pos[:, m0 // 16 : m1 // 16]), bs[:],
-                hw[(b, t)][:, m0:m1], MULT,
-            )
+        def put(m0, m1, b, t, scaled):
+            window = res[(b, t)][:].indirect(pos[:, m0 // PER_COL : m1 // PER_COL])
+            nc.vector.tensor_tensor(window, scaled[:], hw[(b, t)][:, m0:m1], MULT)
+            if m1 == NP:
+                nc.sync.dma_start(out_rows[b, t], res[(b, t)][:])
 
-        def w4_pair(b, tp, a):
-            w4q[(a, b, tp)] = weight_pair(nc.scalar.copy, w4_raw[(a, b)], tp, f"w4q{a}{b}{tp}")
-
-        tiles = [(b, t) for b in range(NB) for t in range(PACK)]
-        vw = []
+        v_s = held([P, S], U8, "v_s")
+        nc.vector.tensor_copy(v_s[:], tab_s[:].indirect(idx[:]))
+        v_w = []
         for jh in range(2):
-            words = held([P, BANK], U32, f"vw{jh}")
-            nc.vector.tensor_copy(words[:], tabw[:].indirect(idx[:, jh * 32 : (jh + 1) * 32]))
-            vw.append(words)
-        w1q[(0, 0)] = weight_pair(nc.vector.tensor_copy, w1_raw[0], 0, "w1q00")
-        w1q[(0, 1)] = weight_pair(nc.scalar.copy, w1_raw[0], 1, "w1q01")
+            v_w.append(held([P, BANK], U32, f"v_w{jh}"))
+            entries = idx[:, jh * BANK // PER_COL : (jh + 1) * BANK // PER_COL]
+            nc.vector.tensor_copy(v_w[jh][:], tab_w[:].indirect(entries))
+        w1_pair(nc.vector.tensor_copy, 0, 0)
+        w1_pair(nc.scalar.copy, 0, 1)
         deal_w2(0, nc.scalar.copy)
-        for i, (b, t) in enumerate(tiles):
+
+        for i in range(len(ROW_TILES)):
             first_stage(i)
             if i == 0:
-                deal_w3s(0)
-                deal_w3s(1)
-            if i == 2:
-                w1q[(1, 0)] = weight_pair(nc.vector.tensor_copy, w1_raw[1], 0, "w1q10")
+                for b in range(NB):
+                    deal_w3_scales(b)
+            if i == PACK - 2:
+                w1_pair(nc.vector.tensor_copy, 1, 0)
                 deal_w2(1, nc.vector.tensor_copy)
-            if i == 4:
-                w1q[(1, 1)] = weight_pair(nc.scalar.copy, w1_raw[1], 1, "w1q11")
-            if i == 4:
-                scale_all(0, 0)
-        pick(len(tiles) - 1)
-        w4_pair(0, 0, 0)
-        w4_pair(0, 0, 1)
-        second_operands(0, 0)
-        deal_w3(0)
-        scale_all(0, 1)
-        second_operands(0, 1)
+            if i == PACK:
+                w1_pair(nc.scalar.copy, 1, 1)
+                scale_all(0)
+            if i == PACK + 1:
+                make_shift(0, 0)
+            if i == PACK + 2:
+                x_quantise("shift", 0, 0)
 
+        w4_quantise(0, 0, 0, w4_round(0, 0, 0))
+        staged_pass_1 = w4_round(1, 0, 0)
+        make_size(0, 0)
+        pick(LAST)
+        make_size(0, 1)
+        deal_w3_words(0)
+        make_shift(0, 1)
+        w4_quantise(1, 0, 0, staged_pass_1)
+        x_quantise("size", 0, 0)
+        x_quantise("shift", 0, 1)
+        x_quantise("size", 0, 1)
+        for b in range(NB):
+            make_size(1, b)
+        scale_all(1)
+        weigh(nc.vector, LAST, stage[("shift", 0, 1)].bitcast(F32))
+        for b in range(NB):
+            make_shift(1, b)
+        for b in range(NB):
+            x_quantise("size", 1, b)
+            x_quantise("shift", 1, b)
 
-        out_rows = out.rearrange("(b p t) j -> b t p j", b=NB, t=PACK)
-        steps = [(hf * HALF, (hf + 1) * HALF, 0, t) for hf in range(2) for t in range(2)]
-        steps += [(0, NP, b, t) for b, t in tiles[2:]]
-        ys = {}
-        for n, (m0, m1, b, t) in enumerate(steps):
-            ys[n] = second_stage(m0, m1, b, t)
-            if n == 0:
-                second_operands(1, 0)
-            if n == 1:
-                second_operands(1, 1)
-                weigh(nc.vector, 7)
-            if n == 2:
-                w4_pair(0, 1, 0)
-                w4_pair(0, 1, 1)
-            if n == 3:
-                scale_all(0, 2)
-            if n == 4:
-                scale_all(0, 3)
-                w4_pair(1, 0, 0)
-                w4_pair(1, 0, 1)
-            if n == 5:
-                deal_w3(1)
-            if n == 6:
-                w4_pair(1, 1, 0)
-                w4_pair(1, 1, 1)
-            if 5 <= n < 9:
-                scale_all(1, n - 5)
-            if n > 0:
-                put(*steps[n - 1], ys[n - 1])
-                if steps[n - 1][1] == NP:
-                    nc.sync.dma_start(out_rows[steps[n - 1][2], steps[n - 1][3]], res[steps[n - 1][2:]][:])
-        put(*steps[-1], ys[len(steps) - 1])
-        nc.sync.dma_start(out_rows[steps[-1][2], steps[-1][3]], res[steps[-1][2:]][:])
+        steps = [(hf * HALF, (hf + 1) * HALF, *ROW_TILES[i]) for hf in range(2) for i in range(2)]
+        steps += [(0, NP, b, t) for b, t in ROW_TILES[2:]]
+        sums = [second_stage(*steps[0]), second_stage(*steps[1])]
+        put(*steps[0], sums[0])
+        staged_pair_1 = [w4_round(a, 0, 1) for a in range(NB)]
+        sums.append(second_stage(*steps[2]))
+        put(*steps[1], sums[1])
+        for a in range(NB):
+            w4_quantise(a, 0, 1, staged_pair_1[a])
+        for n in range(3, len(steps)):
+            sums.append(second_stage(*steps[n]))
+            coming = n - 1
+            if coming == PACK:
+                deal_w3_words(1)
+            if coming == PACK + 1:
+                w4_pair(1, 1)
+            if coming <= LAST:
+                scale_all(coming)
+            if coming == PACK - 1:
+                w4_pair(1, 0)
+            put(*steps[n - 1], sums[n - 1])
+        put(*steps[-1], sums[-1])

@@ -116,9 +116,9 @@ def tile_list_tricot_lapping_inspector_kernel(
         load_per_row(skip_c, skip)
         load_wgo(1)
         load_lap(0, 0)
+        load_w3(0)
         w4_raw = {(a, 0): load_weight(w4, a, 0) for a in range(NB)}
         load_lap(0, 1)
-        load_w3(0)
         for b in range(NB):
             load_lap(1, b)
         for a in range(NB):
@@ -314,12 +314,12 @@ def tile_list_tricot_lapping_inspector_kernel(
             if i == PACK + 2:
                 x_quantise("shift", 0, 0)
 
+        deal_w3_words(0)
         w4_quantise(0, 0, 0, w4_round(0, 0, 0))
         staged_pass_1 = w4_round(1, 0, 0)
         make_size(0, 0)
         pick(LAST)
         make_size(0, 1)
-        deal_w3_words(0)
         make_shift(0, 1)
         w4_quantise(1, 0, 0, staged_pass_1)
         x_quantise("size", 0, 0)

from contextlib import ExitStack

import concourse.mybir as mybir

K, H, T, S, NP = 512, 1024, 2048, 1024, 512
FLOPS = 2 * (2 * K * H * S + 2 * H * H * NP)

F32 = mybir.dt.float32
BF16 = mybir.dt.bfloat16
I32 = mybir.dt.int32
U32 = mybir.dt.uint32
U16 = mybir.dt.uint16
U8 = mybir.dt.uint8
FP8X4 = mybir.dt.float8_e4m3fn_x4
FP4X4 = mybir.dt.float4_e2m1fn_x4
ACT = mybir.ActivationFunctionType
MULT = mybir.AluOpType.mult
ADD = mybir.AluOpType.add

P = 128
PACK = 4
KP = P * PACK
NB = H // KP
BANK = 512
HALF = NP // 2
PAIR = 2 * P
PER_COL = 16
QUADS = 4
ROW_TILES = [(b, t) for b in range(NB) for t in range(PACK)]
LAST = len(ROW_TILES) - 1


def tile_list_tricot_lapping_inspector_kernel(
    tc, tab_words, tab_scales, offs, pos1, w1, w2_words, w2_scales, gain, lap, w3_words, w3_scales, w4, skip, wgo, out
):
    nc = tc.nc
    with ExitStack() as ctx:
        keep = ctx.enter_context(tc.tile_pool(name="keep", bufs=1))
        raw = ctx.enter_context(tc.tile_pool(name="raw", bufs=4))
        ring = ctx.enter_context(tc.tile_pool(name="ring", bufs=2))
        ring3 = ctx.enter_context(tc.tile_pool(name="ring3", bufs=3))
        ps1 = ctx.enter_context(tc.psum_pool(name="ps1", bufs=3))
        ps2 = ctx.enter_context(tc.psum_pool(name="ps2", bufs=2))

        def held(shape, dtype, name):
            return keep.tile(shape, dtype, name=name, align_bytes=64)

        idx = held([P, S // PER_COL], U16, "idx")
        pos = held([P, NP // PER_COL], U16, "pos")
        tab_w = held([P, T], U32, "tab_w")
        tab_s = held([P, T], U8, "tab_s")
        w2_s = held([P, H], U8, "w2_s")
        w3_s = held([P, NB, H], U8, "w3_s")
        w2_w = [held([P, KP], U32, f"w2_w{b}") for b in range(NB)]
        w3_w = [held([P, NB, 2 * KP], U8, f"w3_w{b}") for b in range(NB)]
        gain_c = held([P, NB * PACK], F32, "gain_c")
        skip_c = held([P, NB * PACK], F32, "skip_c")
        lap_t = {(hf, b): held([P, PACK, HALF], F32, f"lap{hf}{b}") for hf in range(2) for b in range(NB)}
        wgo_t = [held([P, 2, NP], F32, f"wgo{tp}") for tp in range(2)]

        nc.gpsimd.memset(tab_s[:].bitcast(I32), 0)
        nc.gpsimd.memset(w2_s[:].bitcast(I32), 0)
        nc.gpsimd.memset(w3_s[:].rearrange("p a c -> p (a c)").bitcast(I32), 0)

        def load_scale_rows(dst, rows, quads):
            for q in quads:
                nc.sync.dma_start(dst[32 * q : 32 * q + 4, :].bitcast(I32), rows[4 * q : 4 * q + 4, :].bitcast(I32))

        def load_weight(w, a, b):
            piece = raw.tile([P, PACK, KP], F32, name="piece")
            nc.sync.dma_start(
                piece[:], w[a * KP : (a + 1) * KP, b * KP : (b + 1) * KP].rearrange("(p j) c -> p j c", j=PACK)
            )
            return piece

        def load_per_row(cols, vec):
            nc.sync.dma_start(
                cols[:].rearrange("p (b t) -> p b t", b=NB), vec.rearrange("(b p t) -> p b t", b=NB, t=PACK)
            )

        def load_w2(b):
            words = w2_words[0].rearrange("p c i -> p (c i)")[:, PACK * b * KP : PACK * (b + 1) * KP]
            nc.sync.dma_start(w2_w[b][:].bitcast(I32), words.bitcast(I32))

        def load_w3(b):
            words = w3_words[:, :, 2 * b * KP : 2 * (b + 1) * KP].rearrange("a p c -> p a c")
            nc.sync.dma_start(w3_w[b][:].bitcast(I32), words.bitcast(I32))

        def load_lap(hf, b):
            rows = lap[b * KP : (b + 1) * KP, hf * HALF : (hf + 1) * HALF]
            nc.sync.dma_start(lap_t[(hf, b)][:], rows.rearrange("(p t) m -> p t m", t=PACK))

        def load_wgo(tp):
            for q in (0, 2, 1, 3):
                nc.sync.dma_start(
                    wgo_t[tp][32 * q : 32 * q + 32], wgo.rearrange("(p t) m -> p t m", t=PACK)[:, 2 * tp : 2 * tp + 2]
                )

        nc.sync.dma_start(idx[:], offs)
        nc.sync.dma_start(pos[:], pos1)
        load_scale_rows(tab_s, tab_scales[0], range(QUADS))
        nc.sync.dma_start(tab_w[:].bitcast(I32), tab_words[0].rearrange("p c i -> p (c i)").bitcast(I32))
        load_scale_rows(w2_s, w2_scales[0], range(1))
        w1_raw = [load_weight(w1, 0, 0)]
        load_w2(0)
        load_scale_rows(w2_s, w2_scales[0], range(1, QUADS))
        load_per_row(gain_c, gain)
        for q in range(QUADS):
            (nc.sync if q < QUADS // 2 else nc.gpsimd).dma_start(
                w3_s[32 * q : 32 * q + 4].bitcast(I32),
                w3_scales[:, 4 * q : 4 * q + 4, :].rearrange("a q c -> q a c").bitcast(I32),
            )
        w1_raw.append(load_weight(w1, 0, 1))
        load_w2(1)
        load_wgo(0)
        load_per_row(skip_c, skip)
        load_wgo(1)
        load_lap(0, 0)
        load_w3(0)
        w4_raw = {(a, 0): load_weight(w4, a, 0) for a in range(NB)}
        load_lap(0, 1)
        for b in range(NB):
            load_lap(1, b)
        for a in range(NB):
            w4_raw[(a, 1)] = load_weight(w4, a, 1)
        load_w3(1)

        def deal(move, dst, src, walk):
            move(dst.rearrange("q a (t p) -> " + walk, t=PACK), src.rearrange("q a (p t) -> " + walk, t=PACK))

        def quantise(staged, width, name):
            codes = held([P, width], U32, name + "c")
            scales = held([P, width], U8, name + "s")
            nc.vector.quantize_mx(out=codes[:].bitcast(FP8X4), scales=scales[:], in_=staged[:])
            return codes, scales

        def round_pair(move, piece, tp):
            staged = ring.tile([P, PACK * PAIR], BF16, name="staged", align_bytes=64, bufs=3)
            move(
                staged[:].rearrange("q (t p j) -> q p j t", t=2, j=PACK),
                piece[:].rearrange("q j (p t) -> q p j t", t=PACK)[:, :, :, 2 * tp : 2 * tp + 2],
            )
            return staged

        w2_sd = [held([P, 1, KP], U8, f"w2_sd{b}") for b in range(NB)]
        w2_wd = [held([P, 1, KP], U32, f"w2_wd{b}") for b in range(NB)]
        w3_sd = [held([P, NB, KP], U8, f"w3_sd{b}") for b in range(NB)]
        w3_wd = [held([P, NB, 2 * KP], U8, f"w3_wd{b}") for b in range(NB)]
        w1q, w4q = {}, {}

        def deal_w2(b, move_words):
            scale_bytes = w2_s[:, b * KP : (b + 1) * KP].rearrange("q (a c) -> q a c", a=1)
            deal(nc.vector.tensor_copy, w2_sd[b][:], scale_bytes, "q a t p")
            deal(move_words, w2_wd[b][:], w2_w[b][:].rearrange("q (a c) -> q a c", a=1), "q a p t")

        def deal_w3_scales(b):
            deal(nc.vector.tensor_copy, w3_sd[b][:], w3_s[:, :, b * KP : (b + 1) * KP], "q a t p")

        def deal_w3_words(b):
            deal(nc.scalar.copy, w3_wd[b][:].bitcast(U16), w3_w[b][:].bitcast(U16), "q a t p")

        def w1_pair(move, b, tp):
            w1q[(b, tp)] = quantise(round_pair(move, w1_raw[b], tp), PAIR, f"w1q{b}{tp}")

        def w4_round(a, b, tp):
            return round_pair(nc.scalar.copy, w4_raw[(a, b)], tp)

        def w4_quantise(a, b, tp, staged):
            w4q[(a, b, tp)] = quantise(staged, PAIR, f"w4q{a}{b}{tp}")

        def w4_pair(b, tp):
            for a in range(NB):
                w4_quantise(a, b, tp, w4_round(a, b, tp))

        def col(cols, b, t):
            return cols[:, b * PACK + t : b * PACK + t + 1]

        h = {}
        hp = [held([P, PACK, NP], F32, f"hp{b}") for b in range(NB)]
        hw = {}

        def weigh(engine, i, where):
            b, t = ROW_TILES[i]
            hw[(b, t)] = where
            engine.tensor_tensor(where, hp[b][:, t, :], wgo_t[t // 2][:, t % 2, :], MULT)

        def pick(i):
            b, t = ROW_TILES[i]
            nc.vector.tensor_copy(hp[b][:, t, :], h[(b, t)][:].indirect(pos[:]))

        def first_stage(i):
            b, t = ROW_TILES[i]
            h[(b, t)] = held([P, S], F32, f"h{b}{t}")
            codes, scales = w1q[(b, t // 2)]
            cols = slice((t % 2) * P, (t % 2 + 1) * P)
            g = col(gain_c, b, t)
            halves = [slice(jh * BANK, (jh + 1) * BANK) for jh in range(2)]
            bent, straight, gbent = [], [], []
            for jh, js in enumerate(halves):
                curve = ps1.tile([P, BANK], F32, name="curve", bufs=2)
                nc.tensor.matmul_mx(
                    out=curve[:], lhsT=codes[:, cols].bitcast(FP8X4), lhsT_scale=scales[:, cols],
                    rhs=v_w[jh][:].bitcast(FP8X4), rhs_scale=v_s[:, js], start=True, stop=True,
                )
                if jh == 0 and i >= 2:
                    bent.append(hp[(i - 1) // PACK][:, (i - 1) % PACK, :])
                else:
                    bent.append(ring.tile([P, BANK], F32, name="bent")[:])
                nc.scalar.activation(bent[jh], curve[:], ACT.Tanh)
            for jh, js in enumerate(halves):
                straight.append(ps1.tile([P, BANK], F32, name="straight", bufs=4))
                nc.tensor.matmul_mx(
                    out=straight[jh][:], lhsT=w2_wd[b][:, 0, t * P : (t + 1) * P].bitcast(FP8X4),
                    lhsT_scale=w2_sd[b][:, 0, t * P : (t + 1) * P],
                    rhs=v_w[jh][:].bitcast(FP8X4), rhs_scale=v_s[:, js], start=True, stop=True,
                )
                gbent.append(ring.tile([P, BANK], F32, name="gbent", bufs=4))
                nc.scalar.activation(gbent[jh][:], bent[jh], ACT.Copy, scale=g)
            if i >= 1:
                pick(i - 1)
                weigh(nc.gpsimd, i - 1, held([P, NP], F32, f"hw{i - 1}")[:])
            for jh, js in enumerate(halves):
                nc.vector.scalar_tensor_tensor(h[(b, t)][:, js], straight[jh][:], g, gbent[jh][:], MULT, ADD)

        width = PACK * HALF
        plain = [held([P, width], BF16, f"stage{n}")[:] for n in range(4)]
        wide = held([P, 2 * width], BF16, "wide")
        stage = {
            ("size", 0, 0): plain[0],
            ("shift", 0, 0): plain[1],
            ("size", 0, 1): wide[:, width // 2 : width // 2 + width],
            ("shift", 0, 1): plain[2],
            ("size", 1, 0): plain[3],
            ("shift", 1, 0): wide[:, :width],
            ("size", 1, 1): plain[1],
            ("shift", 1, 1): wide[:, width:],
        }
        xq = {}
        read_walk, write_walk = "p t (c i) -> p c t i", "p (c i t) -> p c t i"

        def picked(hf, b):
            return hp[b][:, :, hf * HALF : (hf + 1) * HALF].rearrange(read_walk, i=2)

        def make_size(hf, b):
            nc.scalar.activation(stage[("size", hf, b)].rearrange(write_walk, i=2, t=PACK), picked(hf, b), ACT.Abs)

        def make_shift(hf, b):
            laps = lap_t[(hf, b)][:].rearrange(read_walk, i=2)
            woven = stage[("shift", hf, b)].rearrange(write_walk, i=2, t=PACK)
            nc.vector.tensor_tensor(woven, picked(hf, b), laps, ADD)

        def x_quantise(kind, hf, b):
            xq[(kind, hf, b)] = quantise(stage[(kind, hf, b)], HALF, f"{kind}{hf}{b}")

        res = {}
        out_rows = out.rearrange("(b p t) j -> b t p j", b=NB, t=PACK)

        def scale_all(i):
            b, t = ROW_TILES[i]
            res[(b, t)] = ring.tile([P, S], F32, name="res", bufs=4)
            nc.scalar.activation(res[(b, t)][:], h[(b, t)][:], ACT.Copy, scale=col(skip_c, b, t))

        def second_stage(m0, m1, b, t):
            both = ps2.tile([P, m1 - m0], F32, name="both")
            cols = slice((t % 2) * P, (t % 2 + 1) * P)
            for hf in range(m0 // HALF, m1 // HALF):
                ms = slice(hf * HALF - m0, (hf + 1) * HALF - m0)
                for a in range(NB):
                    codes, scales = w4q[(a, b, t // 2)]
                    shift, size = xq[("shift", hf, a)], xq[("size", hf, a)]
                    nc.tensor.matmul_mx(
                        out=both[:, ms], lhsT=codes[:, cols].bitcast(FP8X4), lhsT_scale=scales[:, cols],
                        rhs=shift[0][:].bitcast(FP8X4), rhs_scale=shift[1][:], start=(a == 0), stop=False,
                    )
                    nc.tensor.matmul_mx(
                        out=both[:, ms], lhsT=w3_wd[b][:, a, 2 * t * P : 2 * (t + 1) * P].bitcast(FP4X4),
                        lhsT_scale=w3_sd[b][:, a, t * P : (t + 1) * P],
                        rhs=size[0][:].bitcast(FP8X4), rhs_scale=size[1][:], start=False, stop=(a == NB - 1),
                    )
            scaled = ring3.tile([P, m1 - m0], F32, name="scaled")
            nc.scalar.activation(scaled[:], both[:], ACT.Copy, scale=col(skip_c, b, t))
            return scaled

        def put(m0, m1, b, t, scaled):
            window = res[(b, t)][:].indirect(pos[:, m0 // PER_COL : m1 // PER_COL])
            nc.vector.tensor_tensor(window, scaled[:], hw[(b, t)][:, m0:m1], MULT)
            if m1 == NP:
                nc.sync.dma_start(out_rows[b, t], res[(b, t)][:])

        v_s = held([P, S], U8, "v_s")
        nc.vector.tensor_copy(v_s[:], tab_s[:].indirect(idx[:]))
        v_w = []
        for jh in range(2):
            v_w.append(held([P, BANK], U32, f"v_w{jh}"))
            entries = idx[:, jh * BANK // PER_COL : (jh + 1) * BANK // PER_COL]
            nc.vector.tensor_copy(v_w[jh][:], tab_w[:].indirect(entries))
        w1_pair(nc.vector.tensor_copy, 0, 0)
        w1_pair(nc.scalar.copy, 0, 1)
        deal_w2(0, nc.scalar.copy)

        for i in range(len(ROW_TILES)):
            first_stage(i)
            if i == 0:
                for b in range(NB):
                    deal_w3_scales(b)
            if i == PACK - 2:
                w1_pair(nc.vector.tensor_copy, 1, 0)
                deal_w2(1, nc.vector.tensor_copy)
            if i == PACK:
                w1_pair(nc.scalar.copy, 1, 1)
                scale_all(0)
            if i == PACK + 1:
                make_shift(0, 0)
            if i == PACK + 2:
                x_quantise("shift", 0, 0)

        deal_w3_words(0)
        w4_quantise(0, 0, 0, w4_round(0, 0, 0))
        staged_pass_1 = w4_round(1, 0, 0)
        make_size(0, 0)
        pick(LAST)
        make_size(0, 1)
        make_shift(0, 1)
        w4_quantise(1, 0, 0, staged_pass_1)
        x_quantise("size", 0, 0)
        x_quantise("shift", 0, 1)
        x_quantise("size", 0, 1)
        for b in range(NB):
            make_size(1, b)
        scale_all(1)
        weigh(nc.vector, LAST, stage[("shift", 0, 1)].bitcast(F32))
        for b in range(NB):
            make_shift(1, b)
        for b in range(NB):
            x_quantise("size", 1, b)
            x_quantise("shift", 1, b)

        steps = [(hf * HALF, (hf + 1) * HALF, *ROW_TILES[i]) for hf in range(2) for i in range(2)]
        steps += [(0, NP, b, t) for b, t in ROW_TILES[2:]]
        sums = [second_stage(*steps[0]), second_stage(*steps[1])]
        put(*steps[0], sums[0])
        staged_pair_1 = [w4_round(a, 0, 1) for a in range(NB)]
        sums.append(second_stage(*steps[2]))
        put(*steps[1], sums[1])
        for a in range(NB):
            w4_quantise(a, 0, 1, staged_pair_1[a])
        for n in range(3, len(steps)):
            sums.append(second_stage(*steps[n]))
            coming = n - 1
            if coming == PACK:
                deal_w3_words(1)
            if coming == PACK + 1:
                w4_pair(1, 1)
            if coming <= LAST:
                scale_all(coming)
            if coming == PACK - 1:
                w4_pair(1, 0)
            put(*steps[n - 1], sums[n - 1])
        put(*steps[-1], sums[-1])
